import numpy as np
import ml_dtypes


def mxq(x, axis, fmt="e4m3"):
    dtype, down = {"e4m3": (ml_dtypes.float8_e4m3fn, 7), "e5m2": (ml_dtypes.float8_e5m2, 14)}[fmt]
    v = np.moveaxis(np.asarray(x, np.float32).astype(ml_dtypes.bfloat16).astype(np.float64), axis, -1)
    blocks = v.reshape(v.shape[:-1] + (-1, 32))
    amax = np.abs(blocks).max(-1, keepdims=True)
    byte = np.maximum(np.where(amax > 0, np.frexp(amax)[1] - 1 + 127, 0) - down, 1)
    scale = np.exp2(byte - 127.0)
    codes = (blocks / scale).astype(np.float32).astype(dtype).astype(np.float64)
    return np.moveaxis((codes * scale).reshape(v.shape), -1, axis)


WIDE = False


def mx_kscale(k):
    if not WIDE:
        return np.ones(k)
    levels = np.array([10, -10, 5, -5, 0])
    if k % 512:
        return np.exp2(np.random.permutation(np.resize(levels, k // 32))).repeat(32)
    a = np.empty((k // 512, 16))
    for p in range(k // 512):
        a[p, :8] = np.random.permutation(np.resize(levels, 8))
        for g in range(8):
            far = levels[np.abs(levels - a[p, g]) >= 10]
            a[p, g + 8] = far[np.random.randint(len(far))]
    return np.exp2(a.ravel()).repeat(32)


def f64(x):
    return np.asarray(x).astype(np.float64)


def striped(idx):
    return np.tile(idx.reshape(-1, 16).T, (8, 1)).astype(np.uint16)


def unstriped(offs):
    return offs[:16].T.reshape(-1).astype(np.int64)


E2M1 = np.array([0.0, 0.5, 1.0, 1.5, 2.0, 3.0, 4.0, 6.0, -0.0, -0.5, -1.0, -1.5, -2.0, -3.0, -4.0, -6.0])


def pack_weight(w, fmt):
    k, n = w.shape
    w = f64(np.asarray(w, np.float32).astype(ml_dtypes.bfloat16)).reshape(k // 32, 32, n)
    amax = np.abs(w).max(1)
    if fmt == "e4m3":
        byte = np.frexp(amax)[1] - 1 + 127 - 7
    else:
        mant, ex = np.frexp(amax / 6.0)
        byte = np.where(mant > 0.5, ex, ex - 1) + 127
    byte = np.clip(np.where(amax > 0, byte, 1), 1, 254)
    scaled = (w * np.exp2(127.0 - byte)[:, None, :]).reshape(k, n).astype(np.float32)
    by_word = np.ascontiguousarray(scaled.reshape(k // 512, 128, 4, n).transpose(0, 1, 3, 2))
    if fmt == "e4m3":
        words = by_word.astype(ml_dtypes.float8_e4m3fn).view(np.uint8)
    else:
        c = by_word.astype(ml_dtypes.float4_e2m1fn).view(np.uint8) & 0xF
        words = (c[..., 0::2] | (c[..., 1::2] << 4)).reshape(k // 512, 128, 2 * n)
    return np.ascontiguousarray(words), np.ascontiguousarray(byte.astype(np.uint8).reshape(k // 512, 16, n))


def unpack_weight(words, scales, fmt):
    g, _, n = scales.shape
    words = np.ascontiguousarray(words).reshape(g, 128, n, -1)
    if fmt == "e4m3":
        vals = words.view(ml_dtypes.float8_e4m3fn).astype(np.float64)
    else:
        nib = np.empty((g, 128, n, 4), np.uint8)
        nib[..., 0::2] = words & 0xF
        nib[..., 1::2] = words >> 4
        vals = E2M1[nib]
    vals = vals * np.repeat(np.exp2(scales.astype(np.float64) - 127.0), 8, axis=1)[..., None]
    return vals.transpose(0, 1, 3, 2).reshape(g * 512, n)


def pack_table(v):
    words, scales = pack_weight(v, "e4m3")
    return np.concatenate([words.reshape(words.shape[0], -1), scales.reshape(scales.shape[0], -1)], axis=1)


def unpack_table(tab):
    g, t = tab.shape[0], tab.shape[1] // 528
    return unpack_weight(tab[:, :512 * t].reshape(g, 128, t, 4), tab[:, 512 * t:].reshape(g, 16, t), "e4m3")


def silu(v):
    return v / (1.0 + np.exp(-np.maximum(v, -700.0)))


G, K, M, T, S = 3, 512, 256, 4096, 512


def setup_inputs():
    n = np.random.standard_normal
    s = mx_kscale(K)[:, None]
    p_w4 = pack_weight(n((K, M)) / np.sqrt(K) / s, "e2m1")
    return {
        "tab": pack_table(n((K, T)) * s),
        "w4_words": p_w4[0],
        "w4_scales": p_w4[1],
        "dw": (0.3 * n((K, M)) / np.sqrt(K) / s).astype(np.float32),
        "b": (0.3 * n(256)).astype(np.float32),
        "offs": striped(np.concatenate([np.random.permutation(T)[:S] for _ in range(G)])),
    }


def reference(tab, w4_words, w4_scales, dw, b, offs):
    tab_ = unpack_table(tab)[:, unstriped(offs).reshape(G, S)].sum(1)
    w4_ = unpack_weight(w4_words, w4_scales, "e2m1")
    dw_ = mxq(f64(dw), 0, "e4m3")
    y = tab_.T @ w4_ + tab_.T @ dw_
    return silu(y + f64(b)[None, :])

@@ -1,0 +1,136 @@
+from contextlib import ExitStack
+
+import concourse.mybir as mybir
+from concourse.masks import make_identity
+
+G, K, M, T, S = 3, 512, 256, 4096, 512
+FLOPS = 2 * 2 * G * K * M * S
+
+F32 = mybir.dt.float32
+BF16 = mybir.dt.bfloat16
+I32 = mybir.dt.int32
+U32 = mybir.dt.uint32
+U16 = mybir.dt.uint16
+U8 = mybir.dt.uint8
+FP8X4 = mybir.dt.float8_e4m3fn_x4
+FP4X4 = mybir.dt.float4_e2m1fn_x4
+SILU = mybir.ActivationFunctionType.Silu
+
+P = 128
+PACK = 4
+HALF = 128
+ROWS = 16
+WARM = 48
+
+
+def tile_list_tabbag_tm_sum_silu_kernel(tc, tab, w4_words, w4_scales, dw, b, offs, out):
+    nc = tc.nc
+    with ExitStack() as ctx:
+        sb = ctx.enter_context(tc.tile_pool(name="sb", bufs=1))
+        ps = ctx.enter_context(tc.psum_pool(name="ps", bufs=1))
+
+        offsets = sb.tile([P, G * S // 16], U16, name="offsets")
+        nc.sync.dma_start(offsets[:], offs)
+
+        tab_scales = sb.tile([P, T // 4], I32, name="tab_scales", align_bytes=64)
+        nc.sync.dma_start(
+            tab_scales[P - ROWS : P, :], tab[0, K * T :].rearrange("(q t) -> q t", q=ROWS).bitcast(I32)
+        )
+        nc.vector.memset(tab_scales[0 : P - ROWS, :], 0)
+
+        tab_words = sb.tile([P, T], I32, name="tab_words", align_bytes=64)
+        nc.sync.dma_start(tab_words[:], tab[0, 0 : K * T].rearrange("(p x) -> p x", p=P).bitcast(I32))
+        dw_raw = sb.tile([P, PACK, M], F32, name="dw_raw")
+        nc.sync.dma_start(dw_raw[:], dw.rearrange("(p i) n -> p i n", i=PACK))
+        w4_codes = sb.tile([P, 2 * M // 4], I32, name="w4_codes", align_bytes=64)
+        nc.sync.dma_start(w4_codes[:], w4_words[0].bitcast(I32))
+
+        b_col = sb.tile([P, 2], F32, name="b_col")
+        nc.scalar.dma_start(b_col[:], b.rearrange("(p c) -> p c", c=2))
+        w4_plane = sb.tile([P, M // 4], I32, name="w4_plane", align_bytes=64)
+        nc.gpsimd.memset(w4_plane[:], 0)
+        w4_rows = w4_scales[0].rearrange("(q r) n -> r q n", r=4)
+        for r in range(4):
+            nc.scalar.dma_start(w4_plane[r:P:32, :], w4_rows[r].bitcast(I32))
+        ident = sb.tile([P, P], F32, name="ident")
+        make_identity(nc, ident[:])
+        warm_act = sb.tile([P, 1], F32, name="warm_act")
+        nc.scalar.activation(warm_act[:], b_col[:, 0:1], SILU)
+
+        tab_plane = sb.tile([P, G * S // 4], I32, name="tab_plane", align_bytes=64)
+        nc.vector.memset(tab_plane[:], 0)
+        got_scales = sb.tile([P, G * S // 4], I32, name="got_scales", align_bytes=64)
+        nc.vector.tensor_copy(got_scales[:].bitcast(U8), tab_scales[:].bitcast(U8).indirect(offsets[:]))
+        for r in range(4):
+            nc.scalar.dma_start(tab_plane[r:P:32, :], got_scales[P - ROWS + r : P : 4, :])
+
+        if WARM:
+            warm_ps = ps.tile([P, 4, P], F32, name="warm_ps")
+            for i in range(WARM):
+                nc.tensor.transpose(warm_ps[:, i % 4, :], ident[:], ident[:])
+        b_ps = ps.tile([P, 2, P], F32, name="b_ps")
+        for c in range(2):
+            nc.tensor.transpose(b_ps[:, c, :], b_col[:, c : c + 1].to_broadcast([P, P]), ident[:])
+        bias = sb.tile([P, M], F32, name="bias")
+        nc.scalar.copy(bias[:].rearrange("q (p c) -> q p c", c=2), b_ps[:].rearrange("q c p -> q p c"))
+
+        dw_bf = sb.tile([P, M, PACK], BF16, name="dw_bf", tag="shared", align_bytes=64)
+        got_words = {}
+
+        def gather(g, tag):
+            got_words[g] = sb.tile([P, S], U32, name="got_words%d" % g, tag=tag, align_bytes=64)
+            window = tab_words[:].bitcast(U32)
+            nc.vector.tensor_copy(got_words[g][:], window.indirect(offsets[:, g * S // 16 : (g + 1) * S // 16]))
+
+        acc = [ps.tile([P, M], F32, name="acc%d" % j) for j in range(S // P)]
+        dw_codes = sb.tile([P, M], U32, name="dw_codes", align_bytes=64)
+        dw_plane = sb.tile([P, M], U8, name="dw_plane", align_bytes=64)
+
+        def w4_passes(g, j):
+            for h in range(M // HALF):
+                nc.tensor.matmul_mx(
+                    out=acc[j][:, h * HALF : (h + 1) * HALF],
+                    lhsT=got_words[g][:, j * P : (j + 1) * P].bitcast(FP8X4),
+                    lhsT_scale=tab_plane[:].bitcast(U8)[:, g * S + j * P : g * S + (j + 1) * P],
+                    rhs=w4_codes[:].bitcast(U8)[:, 2 * h * HALF : 2 * (h + 1) * HALF].bitcast(FP4X4),
+                    rhs_scale=w4_plane[:].bitcast(U8)[:, h * HALF : (h + 1) * HALF],
+                    start=(g == 0 and h == 0),
+                    stop=False,
+                )
+
+        def dw_pass(g, j):
+            nc.tensor.matmul_mx(
+                out=acc[j][:],
+                lhsT=got_words[g][:, j * P : (j + 1) * P].bitcast(FP8X4),
+                lhsT_scale=tab_plane[:].bitcast(U8)[:, g * S + j * P : g * S + (j + 1) * P],
+                rhs=dw_codes[:].bitcast(FP8X4),
+                rhs_scale=dw_plane[:],
+                start=False,
+                stop=(g == G - 1),
+            )
+
+        for g in range(G - 1):
+            gather(g, "got_words%d" % g)
+            for j in range(S // P):
+                w4_passes(g, j)
+
+        nc.scalar.copy(
+            dw_bf[:].rearrange("p (c e) i -> p c i e", e=4),
+            dw_raw[:].rearrange("p i (c e) -> p c i e", e=4),
+        )
+        nc.vector.quantize_mx(
+            out=dw_codes[:].bitcast(FP8X4), scales=dw_plane[:], in_=dw_bf[:].rearrange("p n i -> p (n i)")
+        )
+        gather(G - 1, "shared")
+        for g in range(G - 1):
+            for j in range(S // P):
+                dw_pass(g, j)
+
+        for j in range(S // P):
+            w4_passes(G - 1, j)
+            dw_pass(G - 1, j)
+            y = sb.tile([P, M], F32, name="y%d" % j)
+            nc.vector.tensor_tensor(y[:], acc[j][:], bias[:], mybir.AluOpType.add)
+            res = sb.tile([P, M], F32, name="res%d" % j)
+            nc.scalar.activation(res[:], y[:], SILU)
+            nc.sync.dma_start(out[j * P : (j + 1) * P, :], res[:])

@@ -20,7 +20,6 @@ P = 128
 PACK = 4
 HALF = 128
 ROWS = 16
-WARM = 48
 
 
 def tile_list_tabbag_tm_sum_silu_kernel(tc, tab, w4_words, w4_scales, dw, b, offs, out):
@@ -29,106 +28,86 @@ def tile_list_tabbag_tm_sum_silu_kernel(tc, tab, w4_words, w4_scales, dw, b, off
         sb = ctx.enter_context(tc.tile_pool(name="sb", bufs=1))
         ps = ctx.enter_context(tc.psum_pool(name="ps", bufs=1))
 
-        offsets = sb.tile([P, G * S // 16], U16, name="offsets")
-        nc.sync.dma_start(offsets[:], offs)
-
         tab_scales = sb.tile([P, T // 4], I32, name="tab_scales", align_bytes=64)
         nc.sync.dma_start(
             tab_scales[P - ROWS : P, :], tab[0, K * T :].rearrange("(q t) -> q t", q=ROWS).bitcast(I32)
         )
+        offsets = sb.tile([P, G * S // 16], U16, name="offsets")
+        nc.sync.dma_start(offsets[:], offs)
+        staged = sb.tile([P, (G * S + M) // 4], I32, name="staged", align_bytes=64)
+        nc.sync.dma_start(staged[P - ROWS : P, G * S // 4 :], w4_scales[0].bitcast(I32))
         nc.vector.memset(tab_scales[0 : P - ROWS, :], 0)
 
         tab_words = sb.tile([P, T], I32, name="tab_words", align_bytes=64)
         nc.sync.dma_start(tab_words[:], tab[0, 0 : K * T].rearrange("(p x) -> p x", p=P).bitcast(I32))
-        dw_raw = sb.tile([P, PACK, M], F32, name="dw_raw")
-        nc.sync.dma_start(dw_raw[:], dw.rearrange("(p i) n -> p i n", i=PACK))
         w4_codes = sb.tile([P, 2 * M // 4], I32, name="w4_codes", align_bytes=64)
         nc.sync.dma_start(w4_codes[:], w4_words[0].bitcast(I32))
+        dw_raw = sb.tile([P, PACK, M], F32, name="dw_raw")
+        nc.sync.dma_start(dw_raw[:], dw.rearrange("(p i) n -> p i n", i=PACK))
 
         b_col = sb.tile([P, 2], F32, name="b_col")
         nc.scalar.dma_start(b_col[:], b.rearrange("(p c) -> p c", c=2))
-        w4_plane = sb.tile([P, M // 4], I32, name="w4_plane", align_bytes=64)
-        nc.gpsimd.memset(w4_plane[:], 0)
-        w4_rows = w4_scales[0].rearrange("(q r) n -> r q n", r=4)
-        for r in range(4):
-            nc.scalar.dma_start(w4_plane[r:P:32, :], w4_rows[r].bitcast(I32))
+        warm_in = sb.tile([P, 1], F32, name="warm_in")
+        nc.gpsimd.memset(warm_in[:], 0.0)
+        warm_act = sb.tile([P, 1], F32, name="warm_act")
+        nc.scalar.activation(warm_act[:], warm_in[:], SILU)
         ident = sb.tile([P, P], F32, name="ident")
         make_identity(nc, ident[:])
-        warm_act = sb.tile([P, 1], F32, name="warm_act")
-        nc.scalar.activation(warm_act[:], b_col[:, 0:1], SILU)
 
-        tab_plane = sb.tile([P, G * S // 4], I32, name="tab_plane", align_bytes=64)
-        nc.vector.memset(tab_plane[:], 0)
+        plane = sb.tile([P, (G * S + M) // 4], I32, name="plane", align_bytes=64)
+        nc.vector.memset(plane[:], 0)
         got_scales = sb.tile([P, G * S // 4], I32, name="got_scales", align_bytes=64)
         nc.vector.tensor_copy(got_scales[:].bitcast(U8), tab_scales[:].bitcast(U8).indirect(offsets[:]))
+        nc.vector.tensor_copy(staged[:, 0 : G * S // 4], got_scales[:])
         for r in range(4):
-            nc.scalar.dma_start(tab_plane[r:P:32, :], got_scales[P - ROWS + r : P : 4, :])
+            nc.scalar.dma_start(plane[r:P:32, :], staged[P - ROWS + r : P : 4, :])
+        tab_plane = plane[:].bitcast(U8)[:, 0 : G * S]
+        w4_plane = plane[:].bitcast(U8)[:, G * S :]
 
-        if WARM:
-            warm_ps = ps.tile([P, 4, P], F32, name="warm_ps")
-            for i in range(WARM):
-                nc.tensor.transpose(warm_ps[:, i % 4, :], ident[:], ident[:])
         b_ps = ps.tile([P, 2, P], F32, name="b_ps")
         for c in range(2):
             nc.tensor.transpose(b_ps[:, c, :], b_col[:, c : c + 1].to_broadcast([P, P]), ident[:])
         bias = sb.tile([P, M], F32, name="bias")
         nc.scalar.copy(bias[:].rearrange("q (p c) -> q p c", c=2), b_ps[:].rearrange("q c p -> q p c"))
 
-        dw_bf = sb.tile([P, M, PACK], BF16, name="dw_bf", tag="shared", align_bytes=64)
-        got_words = {}
-
-        def gather(g, tag):
-            got_words[g] = sb.tile([P, S], U32, name="got_words%d" % g, tag=tag, align_bytes=64)
-            window = tab_words[:].bitcast(U32)
-            nc.vector.tensor_copy(got_words[g][:], window.indirect(offsets[:, g * S // 16 : (g + 1) * S // 16]))
-
         acc = [ps.tile([P, M], F32, name="acc%d" % j) for j in range(S // P)]
+        got_words = []
+        for g in range(G):
+            got = sb.tile([P, S], U32, name="got_words%d" % g, align_bytes=64)
+            window = tab_words[:].bitcast(U32)
+            nc.vector.tensor_copy(got[:], window.indirect(offsets[:, g * S // 16 : (g + 1) * S // 16]))
+            got_words.append(got)
+            for j in range(S // P):
+                for h in range(M // HALF):
+                    nc.tensor.matmul_mx(
+                        out=acc[j][:, h * HALF : (h + 1) * HALF],
+                        lhsT=got[:, j * P : (j + 1) * P].bitcast(FP8X4),
+                        lhsT_scale=tab_plane[:, g * S + j * P : g * S + (j + 1) * P],
+                        rhs=w4_codes[:].bitcast(U8)[:, 2 * h * HALF : 2 * (h + 1) * HALF].bitcast(FP4X4),
+                        rhs_scale=w4_plane[:, h * HALF : (h + 1) * HALF],
+                        start=(g == 0 and h == 0),
+                        stop=False,
+                    )
+
+        dw_bf = sb.tile([P, M, PACK], BF16, name="dw_bf", align_bytes=64)
         dw_codes = sb.tile([P, M], U32, name="dw_codes", align_bytes=64)
         dw_plane = sb.tile([P, M], U8, name="dw_plane", align_bytes=64)
-
-        def w4_passes(g, j):
-            for h in range(M // HALF):
-                nc.tensor.matmul_mx(
-                    out=acc[j][:, h * HALF : (h + 1) * HALF],
-                    lhsT=got_words[g][:, j * P : (j + 1) * P].bitcast(FP8X4),
-                    lhsT_scale=tab_plane[:].bitcast(U8)[:, g * S + j * P : g * S + (j + 1) * P],
-                    rhs=w4_codes[:].bitcast(U8)[:, 2 * h * HALF : 2 * (h + 1) * HALF].bitcast(FP4X4),
-                    rhs_scale=w4_plane[:].bitcast(U8)[:, h * HALF : (h + 1) * HALF],
-                    start=(g == 0 and h == 0),
-                    stop=False,
-                )
-
-        def dw_pass(g, j):
-            nc.tensor.matmul_mx(
-                out=acc[j][:],
-                lhsT=got_words[g][:, j * P : (j + 1) * P].bitcast(FP8X4),
-                lhsT_scale=tab_plane[:].bitcast(U8)[:, g * S + j * P : g * S + (j + 1) * P],
-                rhs=dw_codes[:].bitcast(FP8X4),
-                rhs_scale=dw_plane[:],
-                start=False,
-                stop=(g == G - 1),
-            )
-
-        for g in range(G - 1):
-            gather(g, "got_words%d" % g)
-            for j in range(S // P):
-                w4_passes(g, j)
-
-        nc.scalar.copy(
-            dw_bf[:].rearrange("p (c e) i -> p c i e", e=4),
-            dw_raw[:].rearrange("p i (c e) -> p c i e", e=4),
-        )
+        nc.scalar.copy(dw_bf[:], dw_raw[:].rearrange("p i n -> p n i"))
         nc.vector.quantize_mx(
             out=dw_codes[:].bitcast(FP8X4), scales=dw_plane[:], in_=dw_bf[:].rearrange("p n i -> p (n i)")
         )
-        gather(G - 1, "shared")
-        for g in range(G - 1):
-            for j in range(S // P):
-                dw_pass(g, j)
 
         for j in range(S // P):
-            w4_passes(G - 1, j)
-            dw_pass(G - 1, j)
+            for g in range(G):
+                nc.tensor.matmul_mx(
+                    out=acc[j][:],
+                    lhsT=got_words[g][:, j * P : (j + 1) * P].bitcast(FP8X4),
+                    lhsT_scale=tab_plane[:, g * S + j * P : g * S + (j + 1) * P],
+                    rhs=dw_codes[:].bitcast(FP8X4),
+                    rhs_scale=dw_plane[:],
+                    start=False,
+                    stop=(g == G - 1),
+                )
             y = sb.tile([P, M], F32, name="y%d" % j)
             nc.vector.tensor_tensor(y[:], acc[j][:], bias[:], mybir.AluOpType.add)
             res = sb.tile([P, M], F32, name="res%d" % j)

@@ -34,8 +34,8 @@ def tile_list_tabbag_tm_sum_silu_kernel(tc, tab, w4_words, w4_scales, dw, b, off
         )
         offsets = sb.tile([P, G * S // 16], U16, name="offsets")
         nc.sync.dma_start(offsets[:], offs)
-        staged = sb.tile([P, (G * S + M) // 4], I32, name="staged", align_bytes=64)
-        nc.sync.dma_start(staged[P - ROWS : P, G * S // 4 :], w4_scales[0].bitcast(I32))
+        staged = sb.tile([P, (S + M) // 4], I32, name="staged", align_bytes=64)
+        nc.sync.dma_start(staged[P - ROWS : P, S // 4 :], w4_scales[0].bitcast(I32))
         nc.vector.memset(tab_scales[0 : P - ROWS, :], 0)
 
         tab_words = sb.tile([P, T], I32, name="tab_words", align_bytes=64)
@@ -54,15 +54,26 @@ def tile_list_tabbag_tm_sum_silu_kernel(tc, tab, w4_words, w4_scales, dw, b, off
         ident = sb.tile([P, P], F32, name="ident")
         make_identity(nc, ident[:])
 
-        plane = sb.tile([P, (G * S + M) // 4], I32, name="plane", align_bytes=64)
-        nc.vector.memset(plane[:], 0)
-        got_scales = sb.tile([P, G * S // 4], I32, name="got_scales", align_bytes=64)
-        nc.vector.tensor_copy(got_scales[:].bitcast(U8), tab_scales[:].bitcast(U8).indirect(offsets[:]))
-        nc.vector.tensor_copy(staged[:, 0 : G * S // 4], got_scales[:])
+        plane_first = sb.tile([P, (S + M) // 4], I32, name="plane_first", align_bytes=64)
+        nc.vector.memset(plane_first[:], 0)
+        plane_rest = sb.tile([P, (G - 1) * S // 4], I32, name="plane_rest", align_bytes=64)
+        nc.vector.memset(plane_rest[:], 0)
+        scale_window = tab_scales[:].bitcast(U8)
+        got_first = sb.tile([P, S // 4], I32, name="got_first", tag="got_scales", align_bytes=64)
+        nc.vector.tensor_copy(got_first[:].bitcast(U8), scale_window.indirect(offsets[:, 0 : S // 16]))
+        nc.vector.tensor_copy(staged[:, 0 : S // 4], got_first[:])
         for r in range(4):
-            nc.scalar.dma_start(plane[r:P:32, :], staged[P - ROWS + r : P : 4, :])
-        tab_plane = plane[:].bitcast(U8)[:, 0 : G * S]
-        w4_plane = plane[:].bitcast(U8)[:, G * S :]
+            nc.scalar.dma_start(plane_first[r:P:32, :], staged[P - ROWS + r : P : 4, :])
+        got_rest = sb.tile([P, (G - 1) * S // 4], I32, name="got_rest", tag="got_scales", align_bytes=64)
+        nc.vector.tensor_copy(got_rest[:].bitcast(U8), scale_window.indirect(offsets[:, S // 16 :]))
+        for r in range(4):
+            nc.sync.dma_start(plane_rest[r:P:32, :], got_rest[P - ROWS + r : P : 4, :])
+        w4_plane = plane_first[:].bitcast(U8)[:, S:]
+
+        def tab_plane(g, j):
+            if g == 0:
+                return plane_first[:].bitcast(U8)[:, j * P : (j + 1) * P]
+            return plane_rest[:].bitcast(U8)[:, (g - 1) * S + j * P : (g - 1) * S + (j + 1) * P]
 
         b_ps = ps.tile([P, 2, P], F32, name="b_ps")
         for c in range(2):
@@ -82,7 +93,7 @@ def tile_list_tabbag_tm_sum_silu_kernel(tc, tab, w4_words, w4_scales, dw, b, off
                     nc.tensor.matmul_mx(
                         out=acc[j][:, h * HALF : (h + 1) * HALF],
                         lhsT=got[:, j * P : (j + 1) * P].bitcast(FP8X4),
-                        lhsT_scale=tab_plane[:, g * S + j * P : g * S + (j + 1) * P],
+                        lhsT_scale=tab_plane(g, j),
                         rhs=w4_codes[:].bitcast(U8)[:, 2 * h * HALF : 2 * (h + 1) * HALF].bitcast(FP4X4),
                         rhs_scale=w4_plane[:, h * HALF : (h + 1) * HALF],
                         start=(g == 0 and h == 0),
@@ -102,7 +113,7 @@ def tile_list_tabbag_tm_sum_silu_kernel(tc, tab, w4_words, w4_scales, dw, b, off
                 nc.tensor.matmul_mx(
                     out=acc[j][:],
                     lhsT=got_words[g][:, j * P : (j + 1) * P].bitcast(FP8X4),
-                    lhsT_scale=tab_plane[:, g * S + j * P : g * S + (j + 1) * P],
+                    lhsT_scale=tab_plane(g, j),
                     rhs=dw_codes[:].bitcast(FP8X4),
                     rhs_scale=dw_plane[:],
                     start=False,

@@ -20,6 +20,7 @@ P = 128
 PACK = 4
 HALF = 128
 ROWS = 16
+FIRST = 2 * S
 
 
 def tile_list_tabbag_tm_sum_silu_kernel(tc, tab, w4_words, w4_scales, dw, b, offs, out):
@@ -34,8 +35,8 @@ def tile_list_tabbag_tm_sum_silu_kernel(tc, tab, w4_words, w4_scales, dw, b, off
         )
         offsets = sb.tile([P, G * S // 16], U16, name="offsets")
         nc.sync.dma_start(offsets[:], offs)
-        staged = sb.tile([P, (S + M) // 4], I32, name="staged", align_bytes=64)
-        nc.sync.dma_start(staged[P - ROWS : P, S // 4 :], w4_scales[0].bitcast(I32))
+        staged = sb.tile([P, (FIRST + M) // 4], I32, name="staged", align_bytes=64)
+        nc.sync.dma_start(staged[P - ROWS : P, FIRST // 4 :], w4_scales[0].bitcast(I32))
         nc.vector.memset(tab_scales[0 : P - ROWS, :], 0)
 
         tab_words = sb.tile([P, T], I32, name="tab_words", align_bytes=64)
@@ -54,26 +55,27 @@ def tile_list_tabbag_tm_sum_silu_kernel(tc, tab, w4_words, w4_scales, dw, b, off
         ident = sb.tile([P, P], F32, name="ident")
         make_identity(nc, ident[:])
 
-        plane_first = sb.tile([P, (S + M) // 4], I32, name="plane_first", align_bytes=64)
+        plane_first = sb.tile([P, (FIRST + M) // 4], I32, name="plane_first", align_bytes=64)
         nc.vector.memset(plane_first[:], 0)
-        plane_rest = sb.tile([P, (G - 1) * S // 4], I32, name="plane_rest", align_bytes=64)
+        plane_rest = sb.tile([P, (G * S - FIRST) // 4], I32, name="plane_rest", align_bytes=64)
         nc.vector.memset(plane_rest[:], 0)
         scale_window = tab_scales[:].bitcast(U8)
-        got_first = sb.tile([P, S // 4], I32, name="got_first", tag="got_scales", align_bytes=64)
-        nc.vector.tensor_copy(got_first[:].bitcast(U8), scale_window.indirect(offsets[:, 0 : S // 16]))
-        nc.vector.tensor_copy(staged[:, 0 : S // 4], got_first[:])
+        got_first = sb.tile([P, FIRST // 4], I32, name="got_first", tag="got_scales", align_bytes=64)
+        nc.vector.tensor_copy(got_first[:].bitcast(U8), scale_window.indirect(offsets[:, 0 : FIRST // 16]))
+        nc.vector.tensor_copy(staged[:, 0 : FIRST // 4], got_first[:])
         for r in range(4):
             nc.scalar.dma_start(plane_first[r:P:32, :], staged[P - ROWS + r : P : 4, :])
-        got_rest = sb.tile([P, (G - 1) * S // 4], I32, name="got_rest", tag="got_scales", align_bytes=64)
-        nc.vector.tensor_copy(got_rest[:].bitcast(U8), scale_window.indirect(offsets[:, S // 16 :]))
+        got_rest = sb.tile([P, (G * S - FIRST) // 4], I32, name="got_rest", tag="got_scales", align_bytes=64)
+        nc.vector.tensor_copy(got_rest[:].bitcast(U8), scale_window.indirect(offsets[:, FIRST // 16 :]))
         for r in range(4):
             nc.sync.dma_start(plane_rest[r:P:32, :], got_rest[P - ROWS + r : P : 4, :])
-        w4_plane = plane_first[:].bitcast(U8)[:, S:]
+        w4_plane = plane_first[:].bitcast(U8)[:, FIRST:]
 
         def tab_plane(g, j):
-            if g == 0:
-                return plane_first[:].bitcast(U8)[:, j * P : (j + 1) * P]
-            return plane_rest[:].bitcast(U8)[:, (g - 1) * S + j * P : (g - 1) * S + (j + 1) * P]
+            m = g * S + j * P
+            if m < FIRST:
+                return plane_first[:].bitcast(U8)[:, m : m + P]
+            return plane_rest[:].bitcast(U8)[:, m - FIRST : m - FIRST + P]
 
         b_ps = ps.tile([P, 2, P], F32, name="b_ps")
         for c in range(2):

@@ -20,13 +20,15 @@ P = 128
 PACK = 4
 HALF = 128
 ROWS = 16
-FIRST = 2 * S
+FIRST = 3 * S // 2
+REST = G * S - FIRST
 
 
 def tile_list_tabbag_tm_sum_silu_kernel(tc, tab, w4_words, w4_scales, dw, b, offs, out):
     nc = tc.nc
     with ExitStack() as ctx:
         sb = ctx.enter_context(tc.tile_pool(name="sb", bufs=1))
+        reuse = ctx.enter_context(tc.tile_pool(name="reuse", bufs=1))
         ps = ctx.enter_context(tc.psum_pool(name="ps", bufs=1))
 
         tab_scales = sb.tile([P, T // 4], I32, name="tab_scales", align_bytes=64)
@@ -43,8 +45,6 @@ def tile_list_tabbag_tm_sum_silu_kernel(tc, tab, w4_words, w4_scales, dw, b, off
         nc.sync.dma_start(tab_words[:], tab[0, 0 : K * T].rearrange("(p x) -> p x", p=P).bitcast(I32))
         w4_codes = sb.tile([P, 2 * M // 4], I32, name="w4_codes", align_bytes=64)
         nc.sync.dma_start(w4_codes[:], w4_words[0].bitcast(I32))
-        dw_raw = sb.tile([P, PACK, M], F32, name="dw_raw")
-        nc.sync.dma_start(dw_raw[:], dw.rearrange("(p i) n -> p i n", i=PACK))
 
         b_col = sb.tile([P, 2], F32, name="b_col")
         nc.scalar.dma_start(b_col[:], b.rearrange("(p c) -> p c", c=2))
@@ -60,12 +60,14 @@ def tile_list_tabbag_tm_sum_silu_kernel(tc, tab, w4_words, w4_scales, dw, b, off
         plane_rest = sb.tile([P, (G * S - FIRST) // 4], I32, name="plane_rest", align_bytes=64)
         nc.vector.memset(plane_rest[:], 0)
         scale_window = tab_scales[:].bitcast(U8)
-        got_first = sb.tile([P, FIRST // 4], I32, name="got_first", tag="got_scales", align_bytes=64)
+        got_first = reuse.tile([P, FIRST // 4], I32, name="got_first", offset=REST - 64)
         nc.vector.tensor_copy(got_first[:].bitcast(U8), scale_window.indirect(offsets[:, 0 : FIRST // 16]))
         nc.vector.tensor_copy(staged[:, 0 : FIRST // 4], got_first[:])
         for r in range(4):
-            nc.scalar.dma_start(plane_first[r:P:32, :], staged[P - ROWS + r : P : 4, :])
-        got_rest = sb.tile([P, (G * S - FIRST) // 4], I32, name="got_rest", tag="got_scales", align_bytes=64)
+            nc.sync.dma_start(plane_first[r:P:32, :], staged[P - ROWS + r : P : 4, :])
+        dw_raw = reuse.tile([P, PACK, M], F32, name="dw_raw", offset=REST)
+        nc.sync.dma_start(dw_raw[:], dw.rearrange("(p i) n -> p i n", i=PACK))
+        got_rest = reuse.tile([P, REST // 4], I32, name="got_rest", offset=0)
         nc.vector.tensor_copy(got_rest[:].bitcast(U8), scale_window.indirect(offsets[:, FIRST // 16 :]))
         for r in range(4):
             nc.sync.dma_start(plane_rest[r:P:32, :], got_rest[P - ROWS + r : P : 4, :])

@@ -46,8 +46,9 @@ def tile_list_tabbag_tm_sum_silu_kernel(tc, tab, w4_words, w4_scales, dw, b, off
         w4_codes = sb.tile([P, 2 * M // 4], I32, name="w4_codes", align_bytes=64)
         nc.sync.dma_start(w4_codes[:], w4_words[0].bitcast(I32))
 
-        b_col = sb.tile([P, 2], F32, name="b_col")
-        nc.scalar.dma_start(b_col[:], b.rearrange("(p c) -> p c", c=2))
+        b_rows = sb.tile([P, P], F32, name="b_rows")
+        nc.scalar.dma_start(b_rows[P - 2 : P, :], b.rearrange("(h n) -> h n", h=2))
+        nc.gpsimd.memset(b_rows[0 : P - 2, :], 0.0)
         warm_in = sb.tile([P, 1], F32, name="warm_in")
         nc.gpsimd.memset(warm_in[:], 0.0)
         warm_act = sb.tile([P, 1], F32, name="warm_act")
@@ -79,28 +80,33 @@ def tile_list_tabbag_tm_sum_silu_kernel(tc, tab, w4_words, w4_scales, dw, b, off
                 return plane_first[:].bitcast(U8)[:, m : m + P]
             return plane_rest[:].bitcast(U8)[:, m - FIRST : m - FIRST + P]
 
-        b_ps = ps.tile([P, 2, P], F32, name="b_ps")
-        for c in range(2):
-            nc.tensor.transpose(b_ps[:, c, :], b_col[:, c : c + 1].to_broadcast([P, P]), ident[:])
+        b_turned = ps.tile([P, P], F32, name="b_turned")
+        nc.tensor.transpose(b_turned[:], b_rows[:], ident[:])
+        b_col = sb.tile([P, 2], F32, name="b_col")
+        nc.scalar.copy(b_col[:], b_turned[:, P - 2 : P])
+        b_ps = ps.tile([P, M], F32, name="b_ps")
+        for h in range(2):
+            nc.tensor.transpose(b_ps[:, h * P : (h + 1) * P], b_col[:, h : h + 1].to_broadcast([P, P]), ident[:])
         bias = sb.tile([P, M], F32, name="bias")
-        nc.scalar.copy(bias[:].rearrange("q (p c) -> q p c", c=2), b_ps[:].rearrange("q c p -> q p c"))
+        nc.scalar.copy(bias[:], b_ps[:])
 
-        acc = [ps.tile([P, M], F32, name="acc%d" % j) for j in range(S // P)]
+        pieces = [(j, 0, M) for j in range(S // P - 1)] + [(S // P - 1, h * HALF, HALF) for h in range(M // HALF)]
+        acc = [ps.tile([P, width], F32, name="acc%d" % i) for i, (j, n0, width) in enumerate(pieces)]
         got_words = []
         for g in range(G):
             got = sb.tile([P, S], U32, name="got_words%d" % g, align_bytes=64)
             window = tab_words[:].bitcast(U32)
             nc.vector.tensor_copy(got[:], window.indirect(offsets[:, g * S // 16 : (g + 1) * S // 16]))
             got_words.append(got)
-            for j in range(S // P):
-                for h in range(M // HALF):
+            for i, (j, n0, width) in enumerate(pieces):
+                for n in range(n0, n0 + width, HALF):
                     nc.tensor.matmul_mx(
-                        out=acc[j][:, h * HALF : (h + 1) * HALF],
+                        out=acc[i][:, n - n0 : n - n0 + HALF],
                         lhsT=got[:, j * P : (j + 1) * P].bitcast(FP8X4),
                         lhsT_scale=tab_plane(g, j),
-                        rhs=w4_codes[:].bitcast(U8)[:, 2 * h * HALF : 2 * (h + 1) * HALF].bitcast(FP4X4),
-                        rhs_scale=w4_plane[:, h * HALF : (h + 1) * HALF],
-                        start=(g == 0 and h == 0),
+                        rhs=w4_codes[:].bitcast(U8)[:, 2 * n : 2 * (n + HALF)].bitcast(FP4X4),
+                        rhs_scale=w4_plane[:, n : n + HALF],
+                        start=(g == 0 and n == n0),
                         stop=False,
                     )
 
@@ -112,19 +118,19 @@ def tile_list_tabbag_tm_sum_silu_kernel(tc, tab, w4_words, w4_scales, dw, b, off
             out=dw_codes[:].bitcast(FP8X4), scales=dw_plane[:], in_=dw_bf[:].rearrange("p n i -> p (n i)")
         )
 
-        for j in range(S // P):
+        for i, (j, n0, width) in enumerate(pieces):
             for g in range(G):
                 nc.tensor.matmul_mx(
-                    out=acc[j][:],
+                    out=acc[i][:],
                     lhsT=got_words[g][:, j * P : (j + 1) * P].bitcast(FP8X4),
                     lhsT_scale=tab_plane(g, j),
-                    rhs=dw_codes[:].bitcast(FP8X4),
-                    rhs_scale=dw_plane[:],
+                    rhs=dw_codes[:, n0 : n0 + width].bitcast(FP8X4),
+                    rhs_scale=dw_plane[:, n0 : n0 + width],
                     start=False,
                     stop=(g == G - 1),
                 )
-            y = sb.tile([P, M], F32, name="y%d" % j)
-            nc.vector.tensor_tensor(y[:], acc[j][:], bias[:], mybir.AluOpType.add)
-            res = sb.tile([P, M], F32, name="res%d" % j)
+            y = sb.tile([P, width], F32, name="y%d" % i)
+            nc.vector.tensor_tensor(y[:], acc[i][:], bias[:, n0 : n0 + width], mybir.AluOpType.add)
+            res = sb.tile([P, width], F32, name="res%d" % i)
             nc.scalar.activation(res[:], y[:], SILU)
-            nc.sync.dma_start(out[j * P : (j + 1) * P, :], res[:])
+            nc.sync.dma_start(out[j * P : (j + 1) * P, n0 : n0 + width], res[:])

@@ -90,7 +90,7 @@ def tile_list_tabbag_tm_sum_silu_kernel(tc, tab, w4_words, w4_scales, dw, b, off
         bias = sb.tile([P, M], F32, name="bias")
         nc.scalar.copy(bias[:], b_ps[:])
 
-        pieces = [(j, 0, M) for j in range(S // P - 1)] + [(S // P - 1, h * HALF, HALF) for h in range(M // HALF)]
+        pieces = [(j, 0, M) for j in range(S // P)]
         acc = [ps.tile([P, width], F32, name="acc%d" % i) for i, (j, n0, width) in enumerate(pieces)]
         got_words = []
         for g in range(G):

@@ -20,7 +20,7 @@ P = 128
 PACK = 4
 HALF = 128
 ROWS = 16
-FIRST = 3 * S // 2
+FIRST = S
 REST = G * S - FIRST
 
 
@@ -61,15 +61,16 @@ def tile_list_tabbag_tm_sum_silu_kernel(tc, tab, w4_words, w4_scales, dw, b, off
         plane_rest = sb.tile([P, (G * S - FIRST) // 4], I32, name="plane_rest", align_bytes=64)
         nc.vector.memset(plane_rest[:], 0)
         scale_window = tab_scales[:].bitcast(U8)
-        got_first = reuse.tile([P, FIRST // 4], I32, name="got_first", offset=REST - 64)
-        nc.vector.tensor_copy(got_first[:].bitcast(U8), scale_window.indirect(offsets[:, 0 : FIRST // 16]))
+        got_first = reuse.tile([P, FIRST // 4], I32, name="got_first", offset=0)
+        nc.vector.tensor_copy(got_first[:].bitcast(U8), scale_window.indirect(offsets[:, 0 : S // 16]))
+        got_rest = sb.tile([P, REST // 4], I32, name="got_rest")
+        nc.vector.tensor_copy(got_rest[:].bitcast(U8)[:, 0:S], scale_window.indirect(offsets[:, S // 16 : 2 * S // 16]))
         nc.vector.tensor_copy(staged[:, 0 : FIRST // 4], got_first[:])
         for r in range(4):
             nc.sync.dma_start(plane_first[r:P:32, :], staged[P - ROWS + r : P : 4, :])
-        dw_raw = reuse.tile([P, PACK, M], F32, name="dw_raw", offset=REST)
+        dw_raw = reuse.tile([P, PACK, M], F32, name="dw_raw", offset=0)
         nc.sync.dma_start(dw_raw[:], dw.rearrange("(p i) n -> p i n", i=PACK))
-        got_rest = reuse.tile([P, REST // 4], I32, name="got_rest", offset=0)
-        nc.vector.tensor_copy(got_rest[:].bitcast(U8), scale_window.indirect(offsets[:, FIRST // 16 :]))
+        nc.vector.tensor_copy(got_rest[:].bitcast(U8)[:, S:], scale_window.indirect(offsets[:, 2 * S // 16 :]))
         for r in range(4):
             nc.sync.dma_start(plane_rest[r:P:32, :], got_rest[P - ROWS + r : P : 4, :])
         w4_plane = plane_first[:].bitcast(U8)[:, FIRST:]

@@ -114,7 +114,9 @@ def tile_list_tabbag_tm_sum_silu_kernel(tc, tab, w4_words, w4_scales, dw, b, off
         dw_bf = sb.tile([P, M, PACK], BF16, name="dw_bf", align_bytes=64)
         dw_codes = sb.tile([P, M], U32, name="dw_codes", align_bytes=64)
         dw_plane = sb.tile([P, M], U8, name="dw_plane", align_bytes=64)
-        nc.scalar.copy(dw_bf[:], dw_raw[:].rearrange("p i n -> p n i"))
+        nc.scalar.copy(
+            dw_bf[:].rearrange("p (c e) i -> p c i e", e=4), dw_raw[:].rearrange("p i (c e) -> p c i e", e=4)
+        )
         nc.vector.quantize_mx(
             out=dw_codes[:].bitcast(FP8X4), scales=dw_plane[:], in_=dw_bf[:].rearrange("p n i -> p (n i)")
         )

@@ -38,7 +38,7 @@ def tile_list_tabbag_tm_sum_silu_kernel(tc, tab, w4_words, w4_scales, dw, b, off
         offsets = sb.tile([P, G * S // 16], U16, name="offsets")
         nc.sync.dma_start(offsets[:], offs)
         staged = sb.tile([P, (FIRST + M) // 4], I32, name="staged", align_bytes=64)
-        nc.sync.dma_start(staged[P - ROWS : P, FIRST // 4 :], w4_scales[0].bitcast(I32))
+        nc.scalar.dma_start(staged[P - ROWS : P, FIRST // 4 :], w4_scales[0].bitcast(I32))
         nc.vector.memset(tab_scales[0 : P - ROWS, :], 0)
 
         tab_words = sb.tile([P, T], I32, name="tab_words", align_bytes=64)
@@ -49,10 +49,6 @@ def tile_list_tabbag_tm_sum_silu_kernel(tc, tab, w4_words, w4_scales, dw, b, off
         b_rows = sb.tile([P, P], F32, name="b_rows")
         nc.scalar.dma_start(b_rows[P - 2 : P, :], b.rearrange("(h n) -> h n", h=2))
         nc.gpsimd.memset(b_rows[0 : P - 2, :], 0.0)
-        warm_in = sb.tile([P, 1], F32, name="warm_in")
-        nc.gpsimd.memset(warm_in[:], 0.0)
-        warm_act = sb.tile([P, 1], F32, name="warm_act")
-        nc.scalar.activation(warm_act[:], warm_in[:], SILU)
         ident = sb.tile([P, P], F32, name="ident")
         make_identity(nc, ident[:])
 

@@ -87,25 +87,30 @@ def tile_list_tabbag_tm_sum_silu_kernel(tc, tab, w4_words, w4_scales, dw, b, off
         bias = sb.tile([P, M], F32, name="bias")
         nc.scalar.copy(bias[:], b_ps[:])
 
-        pieces = [(j, 0, M) for j in range(S // P)]
+        last = S // P - 1
+        pieces = [(j, 0, M) for j in range(last)] + [(last, n0, HALF) for n0 in range(0, M, HALF)]
         acc = [ps.tile([P, width], F32, name="acc%d" % i) for i, (j, n0, width) in enumerate(pieces)]
-        got_words = []
+        got_words = [sb.tile([P, S], U32, name="got_words%d" % g, align_bytes=64) for g in range(G)]
+
+        def w4_passes(g, i):
+            j, n0, width = pieces[i]
+            for n in range(n0, n0 + width, HALF):
+                nc.tensor.matmul_mx(
+                    out=acc[i][:, n - n0 : n - n0 + HALF],
+                    lhsT=got_words[g][:, j * P : (j + 1) * P].bitcast(FP8X4),
+                    lhsT_scale=tab_plane(g, j),
+                    rhs=w4_codes[:].bitcast(U8)[:, 2 * n : 2 * (n + HALF)].bitcast(FP4X4),
+                    rhs_scale=w4_plane[:, n : n + HALF],
+                    start=(g == 0 and n == n0),
+                    stop=False,
+                )
+
         for g in range(G):
-            got = sb.tile([P, S], U32, name="got_words%d" % g, align_bytes=64)
             window = tab_words[:].bitcast(U32)
-            nc.vector.tensor_copy(got[:], window.indirect(offsets[:, g * S // 16 : (g + 1) * S // 16]))
-            got_words.append(got)
+            nc.vector.tensor_copy(got_words[g][:], window.indirect(offsets[:, g * S // 16 : (g + 1) * S // 16]))
             for i, (j, n0, width) in enumerate(pieces):
-                for n in range(n0, n0 + width, HALF):
-                    nc.tensor.matmul_mx(
-                        out=acc[i][:, n - n0 : n - n0 + HALF],
-                        lhsT=got[:, j * P : (j + 1) * P].bitcast(FP8X4),
-                        lhsT_scale=tab_plane(g, j),
-                        rhs=w4_codes[:].bitcast(U8)[:, 2 * n : 2 * (n + HALF)].bitcast(FP4X4),
-                        rhs_scale=w4_plane[:, n : n + HALF],
-                        start=(g == 0 and n == n0),
-                        stop=False,
-                    )
+                if g < G - 1 or j < last:
+                    w4_passes(g, i)
 
         dw_bf = sb.tile([P, M, PACK], BF16, name="dw_bf", align_bytes=64)
         dw_codes = sb.tile([P, M], U32, name="dw_codes", align_bytes=64)
@@ -119,6 +124,8 @@ def tile_list_tabbag_tm_sum_silu_kernel(tc, tab, w4_words, w4_scales, dw, b, off
 
         for i, (j, n0, width) in enumerate(pieces):
             for g in range(G):
+                if g == G - 1 and j == last:
+                    w4_passes(g, i)
                 nc.tensor.matmul_mx(
                     out=acc[i][:],
                     lhsT=got_words[g][:, j * P : (j + 1) * P].bitcast(FP8X4),

@@ -57,15 +57,18 @@ def tile_list_tabbag_tm_sum_silu_kernel(tc, tab, w4_words, w4_scales, dw, b, off
         plane_rest = sb.tile([P, (G * S - FIRST) // 4], I32, name="plane_rest", align_bytes=64)
         nc.vector.memset(plane_rest[:], 0)
         scale_window = tab_scales[:].bitcast(U8)
-        got_first = reuse.tile([P, FIRST // 4], I32, name="got_first", offset=0)
+        got_first = reuse.tile([P, FIRST // 4], I32, name="got_first", offset=PACK * HALF * 4 - 64)
         nc.vector.tensor_copy(got_first[:].bitcast(U8), scale_window.indirect(offsets[:, 0 : S // 16]))
         got_rest = sb.tile([P, REST // 4], I32, name="got_rest")
         nc.vector.tensor_copy(got_rest[:].bitcast(U8)[:, 0:S], scale_window.indirect(offsets[:, S // 16 : 2 * S // 16]))
         nc.vector.tensor_copy(staged[:, 0 : FIRST // 4], got_first[:])
         for r in range(4):
             nc.sync.dma_start(plane_first[r:P:32, :], staged[P - ROWS + r : P : 4, :])
-        dw_raw = reuse.tile([P, PACK, M], F32, name="dw_raw", offset=0)
-        nc.sync.dma_start(dw_raw[:], dw.rearrange("(p i) n -> p i n", i=PACK))
+        dw_raw = []
+        for h in range(2):
+            raw = reuse.tile([P, PACK, HALF], F32, name="dw_raw%d" % h, offset=h * PACK * HALF * 4)
+            nc.sync.dma_start(raw[:], dw.rearrange("(p i) n -> p i n", i=PACK)[:, :, h * HALF : (h + 1) * HALF])
+            dw_raw.append(raw)
         nc.vector.tensor_copy(got_rest[:].bitcast(U8)[:, S:], scale_window.indirect(offsets[:, 2 * S // 16 :]))
         for r in range(4):
             nc.sync.dma_start(plane_rest[r:P:32, :], got_rest[P - ROWS + r : P : 4, :])
@@ -88,55 +91,68 @@ def tile_list_tabbag_tm_sum_silu_kernel(tc, tab, w4_words, w4_scales, dw, b, off
         nc.scalar.copy(bias[:], b_ps[:])
 
         last = S // P - 1
-        pieces = [(j, 0, M) for j in range(last)] + [(last, n0, HALF) for n0 in range(0, M, HALF)]
-        acc = [ps.tile([P, width], F32, name="acc%d" % i) for i, (j, n0, width) in enumerate(pieces)]
-        got_words = [sb.tile([P, S], U32, name="got_words%d" % g, align_bytes=64) for g in range(G)]
+        pieces = [(last, [0])] + [(j, [0, 1]) for j in range(last)] + [(last, [1])]
+        acc = [ps.tile([P, HALF * len(halves)], F32, name="acc%d" % i) for i, (j, halves) in enumerate(pieces)]
+        got_words = [sb.tile([P, S], U32, name="got_words%d" % g, align_bytes=64) for g in range(G - 1)]
+        got_words.append(reuse.tile([P, S], U32, name="got_words_last", align_bytes=64, offset=0))
+        dw_codes = [sb.tile([P, HALF], U32, name="dw_codes%d" % h, align_bytes=64) for h in range(2)]
+        dw_plane = [sb.tile([P, HALF], U8, name="dw_plane%d" % h, align_bytes=64) for h in range(2)]
 
-        def w4_passes(g, i):
-            j, n0, width = pieces[i]
-            for n in range(n0, n0 + width, HALF):
-                nc.tensor.matmul_mx(
-                    out=acc[i][:, n - n0 : n - n0 + HALF],
-                    lhsT=got_words[g][:, j * P : (j + 1) * P].bitcast(FP8X4),
-                    lhsT_scale=tab_plane(g, j),
-                    rhs=w4_codes[:].bitcast(U8)[:, 2 * n : 2 * (n + HALF)].bitcast(FP4X4),
-                    rhs_scale=w4_plane[:, n : n + HALF],
-                    start=(g == 0 and n == n0),
-                    stop=False,
-                )
-
-        for g in range(G):
+        def gather_words(g):
             window = tab_words[:].bitcast(U32)
             nc.vector.tensor_copy(got_words[g][:], window.indirect(offsets[:, g * S // 16 : (g + 1) * S // 16]))
-            for i, (j, n0, width) in enumerate(pieces):
-                if g < G - 1 or j < last:
-                    w4_passes(g, i)
 
-        dw_bf = sb.tile([P, M, PACK], BF16, name="dw_bf", align_bytes=64)
-        dw_codes = sb.tile([P, M], U32, name="dw_codes", align_bytes=64)
-        dw_plane = sb.tile([P, M], U8, name="dw_plane", align_bytes=64)
-        nc.scalar.copy(
-            dw_bf[:].rearrange("p (c e) i -> p c i e", e=4), dw_raw[:].rearrange("p i (c e) -> p c i e", e=4)
-        )
-        nc.vector.quantize_mx(
-            out=dw_codes[:].bitcast(FP8X4), scales=dw_plane[:], in_=dw_bf[:].rearrange("p n i -> p (n i)")
-        )
+        def quantise_dw(h):
+            dw_bf = sb.tile([P, HALF, PACK], BF16, name="dw_bf%d" % h, align_bytes=64)
+            nc.scalar.copy(
+                dw_bf[:].rearrange("p (c e) i -> p c i e", e=4), dw_raw[h][:].rearrange("p i (c e) -> p c i e", e=4)
+            )
+            nc.vector.quantize_mx(
+                out=dw_codes[h][:].bitcast(FP8X4), scales=dw_plane[h][:], in_=dw_bf[:].rearrange("p n i -> p (n i)")
+            )
 
-        for i, (j, n0, width) in enumerate(pieces):
-            for g in range(G):
-                if g == G - 1 and j == last:
-                    w4_passes(g, i)
-                nc.tensor.matmul_mx(
-                    out=acc[i][:],
-                    lhsT=got_words[g][:, j * P : (j + 1) * P].bitcast(FP8X4),
-                    lhsT_scale=tab_plane(g, j),
-                    rhs=dw_codes[:, n0 : n0 + width].bitcast(FP8X4),
-                    rhs_scale=dw_plane[:, n0 : n0 + width],
-                    start=False,
-                    stop=(g == G - 1),
-                )
-            y = sb.tile([P, width], F32, name="y%d" % i)
-            nc.vector.tensor_tensor(y[:], acc[i][:], bias[:, n0 : n0 + width], mybir.AluOpType.add)
-            res = sb.tile([P, width], F32, name="res%d" % i)
+        def mx_pass(g, i, h, codes, plane, start, stop):
+            j, halves = pieces[i]
+            c0 = (h - halves[0]) * HALF
+            nc.tensor.matmul_mx(
+                out=acc[i][:, c0 : c0 + HALF],
+                lhsT=got_words[g][:, j * P : (j + 1) * P].bitcast(FP8X4),
+                lhsT_scale=tab_plane(g, j),
+                rhs=codes,
+                rhs_scale=plane,
+                start=start,
+                stop=stop,
+            )
+
+        def w4_pass(g, i, h):
+            codes = w4_codes[:].bitcast(U8)[:, 2 * h * HALF : 2 * (h + 1) * HALF].bitcast(FP4X4)
+            mx_pass(g, i, h, codes, w4_plane[:, h * HALF : (h + 1) * HALF], g == 0 and h == pieces[i][1][0], False)
+
+        def dw_pass(g, i, h):
+            stop = g == G - 1 and h == pieces[i][1][-1]
+            mx_pass(g, i, h, dw_codes[h][:].bitcast(FP8X4), dw_plane[h][:], False, stop)
+
+        for g in range(G - 1):
+            gather_words(g)
+            for i, (j, halves) in enumerate(pieces):
+                for h in halves:
+                    w4_pass(g, i, h)
+        quantise_dw(0)
+        gather_words(G - 1)
+        for i, (j, halves) in enumerate(pieces):
+            if 0 in halves:
+                for g in range(G - 1):
+                    dw_pass(g, i, 0)
+        quantise_dw(1)
+        for i, (j, halves) in enumerate(pieces):
+            for h in halves:
+                w4_pass(G - 1, i, h)
+            for h in halves:
+                for g in range(G - 1 if h == 0 else 0, G):
+                    dw_pass(g, i, h)
+            cols = slice(halves[0] * HALF, (halves[-1] + 1) * HALF)
+            y = sb.tile([P, HALF * len(halves)], F32, name="y%d" % i)
+            nc.vector.tensor_tensor(y[:], acc[i][:], bias[:, cols], mybir.AluOpType.add)
+            res = sb.tile([P, HALF * len(halves)], F32, name="res%d" % i)
             nc.scalar.activation(res[:], y[:], SILU)
-            nc.sync.dma_start(out[j * P : (j + 1) * P, n0 : n0 + width], res[:])
+            nc.sync.dma_start(out[j * P : (j + 1) * P, cols], res[:])

@@ -22,6 +22,8 @@ HALF = 128
 ROWS = 16
 FIRST = S
 REST = G * S - FIRST
+BANK = 2048
+TILES = S // P
 
 
 def tile_list_tabbag_tm_sum_silu_kernel(tc, tab, w4_words, w4_scales, dw, b, offs, out):
@@ -80,19 +82,20 @@ def tile_list_tabbag_tm_sum_silu_kernel(tc, tab, w4_words, w4_scales, dw, b, off
                 return plane_first[:].bitcast(U8)[:, m : m + P]
             return plane_rest[:].bitcast(U8)[:, m - FIRST : m - FIRST + P]
 
-        b_turned = ps.tile([P, P], F32, name="b_turned")
+        b_turned = ps.tile([P, P], F32, name="b_turned", offset=6 * BANK)
         nc.tensor.transpose(b_turned[:], b_rows[:], ident[:])
         b_col = sb.tile([P, 2], F32, name="b_col")
         nc.scalar.copy(b_col[:], b_turned[:, P - 2 : P])
-        b_ps = ps.tile([P, M], F32, name="b_ps")
+        b_ps = ps.tile([P, M], F32, name="b_ps", offset=7 * BANK)
         for h in range(2):
             nc.tensor.transpose(b_ps[:, h * P : (h + 1) * P], b_col[:, h : h + 1].to_broadcast([P, P]), ident[:])
         bias = sb.tile([P, M], F32, name="bias")
         nc.scalar.copy(bias[:], b_ps[:])
 
-        last = S // P - 1
-        pieces = [(last, [0])] + [(j, [0, 1]) for j in range(last)] + [(last, [1])]
-        acc = [ps.tile([P, HALF * len(halves)], F32, name="acc%d" % i) for i, (j, halves) in enumerate(pieces)]
+        acc = [
+            [ps.tile([P, HALF], F32, name="acc%d_%d" % (h, j), offset=(h * TILES + j) * BANK) for j in range(TILES)]
+            for h in range(2)
+        ]
         got_words = [sb.tile([P, S], U32, name="got_words%d" % g, align_bytes=64) for g in range(G - 1)]
         got_words.append(reuse.tile([P, S], U32, name="got_words_last", align_bytes=64, offset=0))
         dw_codes = [sb.tile([P, HALF], U32, name="dw_codes%d" % h, align_bytes=64) for h in range(2)]
@@ -111,11 +114,9 @@ def tile_list_tabbag_tm_sum_silu_kernel(tc, tab, w4_words, w4_scales, dw, b, off
                 out=dw_codes[h][:].bitcast(FP8X4), scales=dw_plane[h][:], in_=dw_bf[:].rearrange("p n i -> p (n i)")
             )
 
-        def mx_pass(g, i, h, codes, plane, start, stop):
-            j, halves = pieces[i]
-            c0 = (h - halves[0]) * HALF
+        def mx_pass(g, j, h, codes, plane, start, stop):
             nc.tensor.matmul_mx(
-                out=acc[i][:, c0 : c0 + HALF],
+                out=acc[h][j][:],
                 lhsT=got_words[g][:, j * P : (j + 1) * P].bitcast(FP8X4),
                 lhsT_scale=tab_plane(g, j),
                 rhs=codes,
@@ -124,35 +125,39 @@ def tile_list_tabbag_tm_sum_silu_kernel(tc, tab, w4_words, w4_scales, dw, b, off
                 stop=stop,
             )
 
-        def w4_pass(g, i, h):
+        def w4_pass(g, j, h):
             codes = w4_codes[:].bitcast(U8)[:, 2 * h * HALF : 2 * (h + 1) * HALF].bitcast(FP4X4)
-            mx_pass(g, i, h, codes, w4_plane[:, h * HALF : (h + 1) * HALF], g == 0 and h == pieces[i][1][0], False)
+            mx_pass(g, j, h, codes, w4_plane[:, h * HALF : (h + 1) * HALF], g == 0, False)
 
-        def dw_pass(g, i, h):
-            stop = g == G - 1 and h == pieces[i][1][-1]
-            mx_pass(g, i, h, dw_codes[h][:].bitcast(FP8X4), dw_plane[h][:], False, stop)
+        def dw_pass(g, j, h):
+            mx_pass(g, j, h, dw_codes[h][:].bitcast(FP8X4), dw_plane[h][:], False, g == G - 1)
 
         for g in range(G - 1):
             gather_words(g)
-            for i, (j, halves) in enumerate(pieces):
-                for h in halves:
-                    w4_pass(g, i, h)
+            for j in range(TILES):
+                for h in range(2):
+                    w4_pass(g, j, h)
         quantise_dw(0)
         gather_words(G - 1)
-        for i, (j, halves) in enumerate(pieces):
-            if 0 in halves:
-                for g in range(G - 1):
-                    dw_pass(g, i, 0)
+        for j in range(TILES):
+            for g in range(G - 1):
+                dw_pass(g, j, 0)
         quantise_dw(1)
-        for i, (j, halves) in enumerate(pieces):
-            for h in halves:
-                w4_pass(G - 1, i, h)
-            for h in halves:
+        for h in range(2):
+            cols = slice(h * HALF, (h + 1) * HALF)
+            for j in range(TILES):
+                w4_pass(G - 1, j, h)
                 for g in range(G - 1 if h == 0 else 0, G):
-                    dw_pass(g, i, h)
-            cols = slice(halves[0] * HALF, (halves[-1] + 1) * HALF)
-            y = sb.tile([P, HALF * len(halves)], F32, name="y%d" % i)
-            nc.vector.tensor_tensor(y[:], acc[i][:], bias[:, cols], mybir.AluOpType.add)
-            res = sb.tile([P, HALF * len(halves)], F32, name="res%d" % i)
-            nc.scalar.activation(res[:], y[:], SILU)
-            nc.sync.dma_start(out[j * P : (j + 1) * P, cols], res[:])
+                    dw_pass(g, j, h)
+                res = sb.tile([P, HALF], F32, name="res%d_%d" % (h, j))
+                step = HALF // 2 if j == TILES - 1 and h == 1 else HALF
+                for c in range(0, HALF, step):
+                    y = sb.tile([P, step], F32, name="y%d_%d_%d" % (h, j, c))
+                    nc.vector.tensor_tensor(
+                        y[:],
+                        acc[h][j][:, c : c + step],
+                        bias[:, h * HALF + c : h * HALF + c + step],
+                        mybir.AluOpType.add,
+                    )
+                    nc.scalar.activation(res[:, c : c + step], y[:], SILU)
+                nc.sync.dma_start(out[j * P : (j + 1) * P, cols], res[:])

@@ -82,6 +82,8 @@ def tile_list_tabbag_tm_sum_silu_kernel(tc, tab, w4_words, w4_scales, dw, b, off
                 return plane_first[:].bitcast(U8)[:, m : m + P]
             return plane_rest[:].bitcast(U8)[:, m - FIRST : m - FIRST + P]
 
+        table_warm = sb.tile([P, 1], F32, name="table_warm")
+        nc.scalar.activation(table_warm[:], ident[:, 0:1], SILU)
         b_turned = ps.tile([P, P], F32, name="b_turned", offset=6 * BANK)
         nc.tensor.transpose(b_turned[:], b_rows[:], ident[:])
         b_col = sb.tile([P, 2], F32, name="b_col")

@@ -23,6 +23,8 @@ ROWS = 16
 FIRST = S
 REST = G * S - FIRST
 BANK = 2048
+SCALES_AT = 2 * PACK * HALF * 4
+WARM = 4
 TILES = S // P
 
 
@@ -33,7 +35,7 @@ def tile_list_tabbag_tm_sum_silu_kernel(tc, tab, w4_words, w4_scales, dw, b, off
         reuse = ctx.enter_context(tc.tile_pool(name="reuse", bufs=1))
         ps = ctx.enter_context(tc.psum_pool(name="ps", bufs=1))
 
-        tab_scales = sb.tile([P, T // 4], I32, name="tab_scales", align_bytes=64)
+        tab_scales = reuse.tile([P, T // 4], I32, name="tab_scales", align_bytes=64, offset=SCALES_AT)
         nc.sync.dma_start(
             tab_scales[P - ROWS : P, :], tab[0, K * T :].rearrange("(q t) -> q t", q=ROWS).bitcast(I32)
         )
@@ -86,11 +88,14 @@ def tile_list_tabbag_tm_sum_silu_kernel(tc, tab, w4_words, w4_scales, dw, b, off
         nc.scalar.activation(table_warm[:], ident[:, 0:1], SILU)
         b_turned = ps.tile([P, P], F32, name="b_turned", offset=6 * BANK)
         nc.tensor.transpose(b_turned[:], b_rows[:], ident[:])
-        b_col = sb.tile([P, 2], F32, name="b_col")
+        b_col = reuse.tile([P, 2], F32, name="b_col", offset=SCALES_AT)
         nc.scalar.copy(b_col[:], b_turned[:, P - 2 : P])
         b_ps = ps.tile([P, M], F32, name="b_ps", offset=7 * BANK)
         for h in range(2):
             nc.tensor.transpose(b_ps[:, h * P : (h + 1) * P], b_col[:, h : h + 1].to_broadcast([P, P]), ident[:])
+        warm = ps.tile([P, WARM * P], F32, name="warm", offset=6 * BANK)
+        for w in range(WARM):
+            nc.tensor.transpose(warm[:, w * P : (w + 1) * P], b_col[:, 0:1].to_broadcast([P, P]), ident[:])
         bias = sb.tile([P, M], F32, name="bias")
         nc.scalar.copy(bias[:], b_ps[:])
 

@@ -96,6 +96,8 @@ def tile_list_tabbag_tm_sum_silu_kernel(tc, tab, w4_words, w4_scales, dw, b, off
         warm = ps.tile([P, WARM * P], F32, name="warm", offset=6 * BANK)
         for w in range(WARM):
             nc.tensor.transpose(warm[:, w * P : (w + 1) * P], b_col[:, 0:1].to_broadcast([P, P]), ident[:])
+        warm_last = ps.tile([P, P], F32, name="warm_last", offset=5 * BANK)
+        nc.tensor.transpose(warm_last[:], b_col[:, 0:1].to_broadcast([P, P]), ident[:])
         bias = sb.tile([P, M], F32, name="bias")
         nc.scalar.copy(bias[:], b_ps[:])
 

@@ -20,10 +20,11 @@ P = 128
 PACK = 4
 HALF = 128
 ROWS = 16
-FIRST = S
-REST = G * S - FIRST
+PIECE = 256
+EARLY = 2 * S
 BANK = 2048
-SCALES_AT = 2 * PACK * HALF * 4
+RAW = PACK * HALF * 4
+SCALES_AT = 3 * RAW
 WARM = 4
 TILES = S // P
 
@@ -41,8 +42,10 @@ def tile_list_tabbag_tm_sum_silu_kernel(tc, tab, w4_words, w4_scales, dw, b, off
         )
         offsets = sb.tile([P, G * S // 16], U16, name="offsets")
         nc.sync.dma_start(offsets[:], offs)
-        staged = sb.tile([P, (FIRST + M) // 4], I32, name="staged", align_bytes=64)
-        nc.scalar.dma_start(staged[P - ROWS : P, FIRST // 4 :], w4_scales[0].bitcast(I32))
+        staged = sb.tile([P, (EARLY + M) // 4], I32, name="staged", align_bytes=64)
+        nc.scalar.dma_start(staged[P - ROWS : P, EARLY // 4 :], w4_scales[0].bitcast(I32))
+        b_rows = sb.tile([P, P], F32, name="b_rows")
+        nc.scalar.dma_start(b_rows[P - 2 : P, :], b.rearrange("(h n) -> h n", h=2))
         nc.vector.memset(tab_scales[0 : P - ROWS, :], 0)
 
         tab_words = sb.tile([P, T], I32, name="tab_words", align_bytes=64)
@@ -50,39 +53,42 @@ def tile_list_tabbag_tm_sum_silu_kernel(tc, tab, w4_words, w4_scales, dw, b, off
         w4_codes = sb.tile([P, 2 * M // 4], I32, name="w4_codes", align_bytes=64)
         nc.sync.dma_start(w4_codes[:], w4_words[0].bitcast(I32))
 
-        b_rows = sb.tile([P, P], F32, name="b_rows")
-        nc.scalar.dma_start(b_rows[P - 2 : P, :], b.rearrange("(h n) -> h n", h=2))
         nc.gpsimd.memset(b_rows[0 : P - 2, :], 0.0)
         ident = sb.tile([P, P], F32, name="ident")
         make_identity(nc, ident[:])
 
-        plane_first = sb.tile([P, (FIRST + M) // 4], I32, name="plane_first", align_bytes=64)
-        nc.vector.memset(plane_first[:], 0)
-        plane_rest = sb.tile([P, (G * S - FIRST) // 4], I32, name="plane_rest", align_bytes=64)
-        nc.vector.memset(plane_rest[:], 0)
+        plane_early = sb.tile([P, (EARLY + M) // 4], I32, name="plane_early", align_bytes=64)
+        nc.vector.memset(plane_early[:], 0)
+        plane_late = sb.tile([P, S // 4], I32, name="plane_late", align_bytes=64)
+        nc.vector.memset(plane_late[:], 0)
         scale_window = tab_scales[:].bitcast(U8)
-        got_first = reuse.tile([P, FIRST // 4], I32, name="got_first", offset=PACK * HALF * 4 - 64)
-        nc.vector.tensor_copy(got_first[:].bitcast(U8), scale_window.indirect(offsets[:, 0 : S // 16]))
-        got_rest = sb.tile([P, REST // 4], I32, name="got_rest")
-        nc.vector.tensor_copy(got_rest[:].bitcast(U8)[:, 0:S], scale_window.indirect(offsets[:, S // 16 : 2 * S // 16]))
-        nc.vector.tensor_copy(staged[:, 0 : FIRST // 4], got_first[:])
+
+        def list_slice(first, count):
+            return offsets[:, first // 16 : (first + count) // 16]
+
+        got = [reuse.tile([P, S // 4], I32, name="got%d" % g, offset=g * (2 * RAW - 64)) for g in range(G - 1)]
+        for g in range(G - 1):
+            nc.vector.tensor_copy(got[g][:].bitcast(U8), scale_window.indirect(list_slice(g * S, S)))
+        for g in range(G - 1):
+            nc.vector.tensor_copy(staged[:, g * S // 4 : (g + 1) * S // 4], got[g][:])
         for r in range(4):
-            nc.sync.dma_start(plane_first[r:P:32, :], staged[P - ROWS + r : P : 4, :])
+            nc.sync.dma_start(plane_early[r:P:32, :], staged[P - ROWS + r : P : 4, :])
+        got_last = reuse.tile([P, S // 4], I32, name="got_last", offset=0)
+        nc.vector.tensor_copy(got_last[:].bitcast(U8), scale_window.indirect(list_slice((G - 1) * S, S)))
         dw_raw = []
         for h in range(2):
-            raw = reuse.tile([P, PACK, HALF], F32, name="dw_raw%d" % h, offset=h * PACK * HALF * 4)
+            raw = reuse.tile([P, PACK, HALF], F32, name="dw_raw%d" % h, offset=(h + 1) * RAW)
             nc.sync.dma_start(raw[:], dw.rearrange("(p i) n -> p i n", i=PACK)[:, :, h * HALF : (h + 1) * HALF])
             dw_raw.append(raw)
-        nc.vector.tensor_copy(got_rest[:].bitcast(U8)[:, S:], scale_window.indirect(offsets[:, 2 * S // 16 :]))
         for r in range(4):
-            nc.sync.dma_start(plane_rest[r:P:32, :], got_rest[P - ROWS + r : P : 4, :])
-        w4_plane = plane_first[:].bitcast(U8)[:, FIRST:]
+            nc.sync.dma_start(plane_late[r:P:32, :], got_last[P - ROWS + r : P : 4, :])
+        w4_plane = plane_early[:].bitcast(U8)[:, EARLY:]
 
         def tab_plane(g, j):
             m = g * S + j * P
-            if m < FIRST:
-                return plane_first[:].bitcast(U8)[:, m : m + P]
-            return plane_rest[:].bitcast(U8)[:, m - FIRST : m - FIRST + P]
+            if m < EARLY:
+                return plane_early[:].bitcast(U8)[:, m : m + P]
+            return plane_late[:].bitcast(U8)[:, m - EARLY : m - EARLY + P]
 
         table_warm = sb.tile([P, 1], F32, name="table_warm")
         nc.scalar.activation(table_warm[:], ident[:, 0:1], SILU)
@@ -105,14 +111,18 @@ def tile_list_tabbag_tm_sum_silu_kernel(tc, tab, w4_words, w4_scales, dw, b, off
             [ps.tile([P, HALF], F32, name="acc%d_%d" % (h, j), offset=(h * TILES + j) * BANK) for j in range(TILES)]
             for h in range(2)
         ]
-        got_words = [sb.tile([P, S], U32, name="got_words%d" % g, align_bytes=64) for g in range(G - 1)]
-        got_words.append(reuse.tile([P, S], U32, name="got_words_last", align_bytes=64, offset=0))
+        words = {}
         dw_codes = [sb.tile([P, HALF], U32, name="dw_codes%d" % h, align_bytes=64) for h in range(2)]
         dw_plane = [sb.tile([P, HALF], U8, name="dw_plane%d" % h, align_bytes=64) for h in range(2)]
 
-        def gather_words(g):
-            window = tab_words[:].bitcast(U32)
-            nc.vector.tensor_copy(got_words[g][:], window.indirect(offsets[:, g * S // 16 : (g + 1) * S // 16]))
+        def gather_words(g, u):
+            if g < G - 1:
+                piece = sb.tile([P, PIECE], U32, name="words%d_%d" % (g, u), align_bytes=64)
+            else:
+                piece = reuse.tile([P, PIECE], U32, name="words_last%d" % u, align_bytes=64, offset=RAW + u * PIECE * 4)
+            nc.vector.tensor_copy(piece[:], tab_words[:].bitcast(U32).indirect(list_slice(g * S + u * PIECE, PIECE)))
+            for e in range(PIECE // P):
+                words[g, u * (PIECE // P) + e] = piece[:, e * P : (e + 1) * P].bitcast(FP8X4)
 
         def quantise_dw(h):
             dw_bf = sb.tile([P, HALF, PACK], BF16, name="dw_bf%d" % h, align_bytes=64)
@@ -126,7 +136,7 @@ def tile_list_tabbag_tm_sum_silu_kernel(tc, tab, w4_words, w4_scales, dw, b, off
         def mx_pass(g, j, h, codes, plane, start, stop):
             nc.tensor.matmul_mx(
                 out=acc[h][j][:],
-                lhsT=got_words[g][:, j * P : (j + 1) * P].bitcast(FP8X4),
+                lhsT=words[g, j],
                 lhsT_scale=tab_plane(g, j),
                 rhs=codes,
                 rhs_scale=plane,
@@ -141,32 +151,37 @@ def tile_list_tabbag_tm_sum_silu_kernel(tc, tab, w4_words, w4_scales, dw, b, off
         def dw_pass(g, j, h):
             mx_pass(g, j, h, dw_codes[h][:].bitcast(FP8X4), dw_plane[h][:], False, g == G - 1)
 
-        for g in range(G - 1):
-            gather_words(g)
-            for j in range(TILES):
-                for h in range(2):
-                    w4_pass(g, j, h)
+        def finish(j, h, step):
+            res = sb.tile([P, HALF], F32, name="res%d_%d" % (h, j))
+            for c in range(0, HALF, step):
+                y = sb.tile([P, step], F32, name="y%d_%d_%d" % (h, j, c))
+                nc.vector.tensor_tensor(
+                    y[:], acc[h][j][:, c : c + step], bias[:, h * HALF + c : h * HALF + c + step], mybir.AluOpType.add
+                )
+                nc.scalar.activation(res[:, c : c + step], y[:], SILU)
+            nc.sync.dma_start(out[j * P : (j + 1) * P, h * HALF : (h + 1) * HALF], res[:])
+
+        for u in range(S // PIECE):
+            for g in range(G - 1):
+                gather_words(g, u)
+                for j in range(2 * u, 2 * u + 2):
+                    for h in range(2):
+                        w4_pass(g, j, h)
         quantise_dw(0)
-        gather_words(G - 1)
         for j in range(TILES):
             for g in range(G - 1):
                 dw_pass(g, j, 0)
+        for u in range(S // PIECE):
+            gather_words(G - 1, u)
         quantise_dw(1)
-        for h in range(2):
-            cols = slice(h * HALF, (h + 1) * HALF)
-            for j in range(TILES):
-                w4_pass(G - 1, j, h)
-                for g in range(G - 1 if h == 0 else 0, G):
-                    dw_pass(g, j, h)
-                res = sb.tile([P, HALF], F32, name="res%d_%d" % (h, j))
-                step = HALF // 2 if j == TILES - 1 and h == 1 else HALF
-                for c in range(0, HALF, step):
-                    y = sb.tile([P, step], F32, name="y%d_%d_%d" % (h, j, c))
-                    nc.vector.tensor_tensor(
-                        y[:],
-                        acc[h][j][:, c : c + step],
-                        bias[:, h * HALF + c : h * HALF + c + step],
-                        mybir.AluOpType.add,
-                    )
-                    nc.scalar.activation(res[:, c : c + step], y[:], SILU)
-                nc.sync.dma_start(out[j * P : (j + 1) * P, cols], res[:])
+        for u in range(S // PIECE):
+            for j in range(2 * u, 2 * u + 2):
+                w4_pass(G - 1, j, 0)
+                dw_pass(G - 1, j, 0)
+                finish(j, 0, HALF)
+            for j in range(2 * u, 2 * u + 2):
+                w4_pass(G - 1, j, 1)
+        for j in range(TILES):
+            for g in range(G):
+                dw_pass(g, j, 1)
+            finish(j, 1, HALF // 2 if j == TILES - 1 else HALF)

@@ -42,8 +42,6 @@ def tile_list_tabbag_tm_sum_silu_kernel(tc, tab, w4_words, w4_scales, dw, b, off
         )
         offsets = sb.tile([P, G * S // 16], U16, name="offsets")
         nc.sync.dma_start(offsets[:], offs)
-        staged = sb.tile([P, (EARLY + M) // 4], I32, name="staged", align_bytes=64)
-        nc.scalar.dma_start(staged[P - ROWS : P, EARLY // 4 :], w4_scales[0].bitcast(I32))
         b_rows = sb.tile([P, P], F32, name="b_rows")
         nc.scalar.dma_start(b_rows[P - 2 : P, :], b.rearrange("(h n) -> h n", h=2))
         nc.vector.memset(tab_scales[0 : P - ROWS, :], 0)
@@ -56,8 +54,12 @@ def tile_list_tabbag_tm_sum_silu_kernel(tc, tab, w4_words, w4_scales, dw, b, off
         nc.gpsimd.memset(b_rows[0 : P - 2, :], 0.0)
         ident = sb.tile([P, P], F32, name="ident")
         make_identity(nc, ident[:])
+        w4_rows = sb.tile([P, M // 4], I32, name="w4_rows", align_bytes=64)
+        nc.gpsimd.memset(w4_rows[:], 0)
+        for q in range(4):
+            nc.gpsimd.dma_start(w4_rows[32 * q : 32 * q + 4, :], w4_scales[0, 4 * q : 4 * q + 4, :].bitcast(I32))
 
-        plane_early = sb.tile([P, (EARLY + M) // 4], I32, name="plane_early", align_bytes=64)
+        plane_early = sb.tile([P, EARLY // 4], I32, name="plane_early", align_bytes=64)
         nc.vector.memset(plane_early[:], 0)
         plane_late = sb.tile([P, S // 4], I32, name="plane_late", align_bytes=64)
         nc.vector.memset(plane_late[:], 0)
@@ -66,14 +68,11 @@ def tile_list_tabbag_tm_sum_silu_kernel(tc, tab, w4_words, w4_scales, dw, b, off
         def list_slice(first, count):
             return offsets[:, first // 16 : (first + count) // 16]
 
-        got = [reuse.tile([P, S // 4], I32, name="got%d" % g, offset=g * (2 * RAW - 64)) for g in range(G - 1)]
-        for g in range(G - 1):
-            nc.vector.tensor_copy(got[g][:].bitcast(U8), scale_window.indirect(list_slice(g * S, S)))
-        for g in range(G - 1):
-            nc.vector.tensor_copy(staged[:, g * S // 4 : (g + 1) * S // 4], got[g][:])
+        got_early = sb.tile([P, EARLY // 4], I32, name="got_early")
+        nc.vector.tensor_copy(got_early[:].bitcast(U8), scale_window.indirect(list_slice(0, EARLY)))
         for r in range(4):
-            nc.sync.dma_start(plane_early[r:P:32, :], staged[P - ROWS + r : P : 4, :])
-        got_last = reuse.tile([P, S // 4], I32, name="got_last", offset=0)
+            nc.sync.dma_start(plane_early[r:P:32, :], got_early[P - ROWS + r : P : 4, :])
+        got_last = sb.tile([P, S // 4], I32, name="got_last")
         nc.vector.tensor_copy(got_last[:].bitcast(U8), scale_window.indirect(list_slice((G - 1) * S, S)))
         dw_raw = []
         for h in range(2):
@@ -82,7 +81,7 @@ def tile_list_tabbag_tm_sum_silu_kernel(tc, tab, w4_words, w4_scales, dw, b, off
             dw_raw.append(raw)
         for r in range(4):
             nc.sync.dma_start(plane_late[r:P:32, :], got_last[P - ROWS + r : P : 4, :])
-        w4_plane = plane_early[:].bitcast(U8)[:, EARLY:]
+        w4_plane = w4_rows[:].bitcast(U8)
 
         def tab_plane(g, j):
             m = g * S + j * P

@@ -25,7 +25,6 @@ EARLY = 2 * S
 BANK = 2048
 RAW = PACK * HALF * 4
 SCALES_AT = 3 * RAW
-WARM = 4
 TILES = S // P
 
 
@@ -98,11 +97,6 @@ def tile_list_tabbag_tm_sum_silu_kernel(tc, tab, w4_words, w4_scales, dw, b, off
         b_ps = ps.tile([P, M], F32, name="b_ps", offset=7 * BANK)
         for h in range(2):
             nc.tensor.transpose(b_ps[:, h * P : (h + 1) * P], b_col[:, h : h + 1].to_broadcast([P, P]), ident[:])
-        warm = ps.tile([P, WARM * P], F32, name="warm", offset=6 * BANK)
-        for w in range(WARM):
-            nc.tensor.transpose(warm[:, w * P : (w + 1) * P], b_col[:, 0:1].to_broadcast([P, P]), ident[:])
-        warm_last = ps.tile([P, P], F32, name="warm_last", offset=5 * BANK)
-        nc.tensor.transpose(warm_last[:], b_col[:, 0:1].to_broadcast([P, P]), ident[:])
         bias = sb.tile([P, M], F32, name="bias")
         nc.scalar.copy(bias[:], b_ps[:])
 

@@ -21,7 +21,8 @@ PACK = 4
 HALF = 128
 ROWS = 16
 PIECE = 256
-EARLY = 2 * S
+EARLY = S + PIECE
+LATE = G * S - EARLY
 BANK = 2048
 RAW = PACK * HALF * 4
 SCALES_AT = 3 * RAW
@@ -41,6 +42,13 @@ def tile_list_tabbag_tm_sum_silu_kernel(tc, tab, w4_words, w4_scales, dw, b, off
         )
         offsets = sb.tile([P, G * S // 16], U16, name="offsets")
         nc.sync.dma_start(offsets[:], offs)
+        w4_rows = sb.tile([P, M // 4], I32, name="w4_rows", align_bytes=64)
+        nc.gpsimd.memset(w4_rows[:], 0)
+
+        def load_w4_rows(queue, q):
+            queue.dma_start(w4_rows[32 * q : 32 * q + 4, :], w4_scales[0, 4 * q : 4 * q + 4, :].bitcast(I32))
+
+        load_w4_rows(nc.scalar, 0)
         b_rows = sb.tile([P, P], F32, name="b_rows")
         nc.scalar.dma_start(b_rows[P - 2 : P, :], b.rearrange("(h n) -> h n", h=2))
         nc.vector.memset(tab_scales[0 : P - ROWS, :], 0)
@@ -53,14 +61,12 @@ def tile_list_tabbag_tm_sum_silu_kernel(tc, tab, w4_words, w4_scales, dw, b, off
         nc.gpsimd.memset(b_rows[0 : P - 2, :], 0.0)
         ident = sb.tile([P, P], F32, name="ident")
         make_identity(nc, ident[:])
-        w4_rows = sb.tile([P, M // 4], I32, name="w4_rows", align_bytes=64)
-        nc.gpsimd.memset(w4_rows[:], 0)
-        for q in range(4):
-            nc.gpsimd.dma_start(w4_rows[32 * q : 32 * q + 4, :], w4_scales[0, 4 * q : 4 * q + 4, :].bitcast(I32))
+        for q in range(1, 4):
+            load_w4_rows(nc.gpsimd, q)
 
         plane_early = sb.tile([P, EARLY // 4], I32, name="plane_early", align_bytes=64)
         nc.vector.memset(plane_early[:], 0)
-        plane_late = sb.tile([P, S // 4], I32, name="plane_late", align_bytes=64)
+        plane_late = sb.tile([P, LATE // 4], I32, name="plane_late", align_bytes=64)
         nc.vector.memset(plane_late[:], 0)
         scale_window = tab_scales[:].bitcast(U8)
 
@@ -71,15 +77,14 @@ def tile_list_tabbag_tm_sum_silu_kernel(tc, tab, w4_words, w4_scales, dw, b, off
         nc.vector.tensor_copy(got_early[:].bitcast(U8), scale_window.indirect(list_slice(0, EARLY)))
         for r in range(4):
             nc.sync.dma_start(plane_early[r:P:32, :], got_early[P - ROWS + r : P : 4, :])
-        got_last = sb.tile([P, S // 4], I32, name="got_last")
-        nc.vector.tensor_copy(got_last[:].bitcast(U8), scale_window.indirect(list_slice((G - 1) * S, S)))
-        dw_raw = []
-        for h in range(2):
-            raw = reuse.tile([P, PACK, HALF], F32, name="dw_raw%d" % h, offset=(h + 1) * RAW)
-            nc.sync.dma_start(raw[:], dw.rearrange("(p i) n -> p i n", i=PACK)[:, :, h * HALF : (h + 1) * HALF])
-            dw_raw.append(raw)
+        got_late = sb.tile([P, LATE // 4], I32, name="got_late")
+        nc.vector.tensor_copy(got_late[:].bitcast(U8), scale_window.indirect(list_slice(EARLY, LATE)))
+        dw_raw = [reuse.tile([P, PACK, HALF], F32, name="dw_raw%d" % h, offset=(h + 1) * RAW) for h in range(2)]
+        dw_rows = dw.rearrange("(p i) n -> p i n", i=PACK)
+        nc.sync.dma_start(dw_raw[0][:], dw_rows[:, :, 0:HALF])
         for r in range(4):
-            nc.sync.dma_start(plane_late[r:P:32, :], got_last[P - ROWS + r : P : 4, :])
+            nc.sync.dma_start(plane_late[r:P:32, :], got_late[P - ROWS + r : P : 4, :])
+        nc.sync.dma_start(dw_raw[1][:], dw_rows[:, :, HALF:])
         w4_plane = w4_rows[:].bitcast(U8)
 
         def tab_plane(g, j):
@@ -147,7 +152,10 @@ def tile_list_tabbag_tm_sum_silu_kernel(tc, tab, w4_words, w4_scales, dw, b, off
         def finish(j, h, step):
             res = sb.tile([P, HALF], F32, name="res%d_%d" % (h, j))
             for c in range(0, HALF, step):
-                y = sb.tile([P, step], F32, name="y%d_%d_%d" % (h, j, c))
+                if h == 0:
+                    y = reuse.tile([P, step], F32, name="y_first%d" % j, offset=2 * RAW + j * HALF * 4)
+                else:
+                    y = sb.tile([P, step], F32, name="y%d_%d" % (j, c))
                 nc.vector.tensor_tensor(
                     y[:], acc[h][j][:, c : c + step], bias[:, h * HALF + c : h * HALF + c + step], mybir.AluOpType.add
                 )

@@ -42,13 +42,8 @@ def tile_list_tabbag_tm_sum_silu_kernel(tc, tab, w4_words, w4_scales, dw, b, off
         )
         offsets = sb.tile([P, G * S // 16], U16, name="offsets")
         nc.sync.dma_start(offsets[:], offs)
-        w4_rows = sb.tile([P, M // 4], I32, name="w4_rows", align_bytes=64)
-        nc.gpsimd.memset(w4_rows[:], 0)
-
-        def load_w4_rows(queue, q):
-            queue.dma_start(w4_rows[32 * q : 32 * q + 4, :], w4_scales[0, 4 * q : 4 * q + 4, :].bitcast(I32))
-
-        load_w4_rows(nc.scalar, 0)
+        staged = sb.tile([P, (EARLY + M) // 4], I32, name="staged")
+        nc.scalar.dma_start(staged[P - ROWS : P, EARLY // 4 :], w4_scales[0].bitcast(I32))
         b_rows = sb.tile([P, P], F32, name="b_rows")
         nc.scalar.dma_start(b_rows[P - 2 : P, :], b.rearrange("(h n) -> h n", h=2))
         nc.vector.memset(tab_scales[0 : P - ROWS, :], 0)
@@ -61,10 +56,8 @@ def tile_list_tabbag_tm_sum_silu_kernel(tc, tab, w4_words, w4_scales, dw, b, off
         nc.gpsimd.memset(b_rows[0 : P - 2, :], 0.0)
         ident = sb.tile([P, P], F32, name="ident")
         make_identity(nc, ident[:])
-        for q in range(1, 4):
-            load_w4_rows(nc.gpsimd, q)
 
-        plane_early = sb.tile([P, EARLY // 4], I32, name="plane_early", align_bytes=64)
+        plane_early = sb.tile([P, (EARLY + M) // 4], I32, name="plane_early", align_bytes=64)
         nc.vector.memset(plane_early[:], 0)
         plane_late = sb.tile([P, LATE // 4], I32, name="plane_late", align_bytes=64)
         nc.vector.memset(plane_late[:], 0)
@@ -73,11 +66,12 @@ def tile_list_tabbag_tm_sum_silu_kernel(tc, tab, w4_words, w4_scales, dw, b, off
         def list_slice(first, count):
             return offsets[:, first // 16 : (first + count) // 16]
 
-        got_early = sb.tile([P, EARLY // 4], I32, name="got_early")
+        got_early = reuse.tile([P, EARLY // 4], I32, name="got_early", offset=0)
         nc.vector.tensor_copy(got_early[:].bitcast(U8), scale_window.indirect(list_slice(0, EARLY)))
+        nc.vector.tensor_copy(staged[96:P, 0 : EARLY // 4], got_early[96:P, :])
         for r in range(4):
-            nc.sync.dma_start(plane_early[r:P:32, :], got_early[P - ROWS + r : P : 4, :])
-        got_late = sb.tile([P, LATE // 4], I32, name="got_late")
+            nc.sync.dma_start(plane_early[r:P:32, :], staged[P - ROWS + r : P : 4, :])
+        got_late = reuse.tile([P, LATE // 4], I32, name="got_late", offset=0)
         nc.vector.tensor_copy(got_late[:].bitcast(U8), scale_window.indirect(list_slice(EARLY, LATE)))
         dw_raw = [reuse.tile([P, PACK, HALF], F32, name="dw_raw%d" % h, offset=(h + 1) * RAW) for h in range(2)]
         dw_rows = dw.rearrange("(p i) n -> p i n", i=PACK)
@@ -85,7 +79,7 @@ def tile_list_tabbag_tm_sum_silu_kernel(tc, tab, w4_words, w4_scales, dw, b, off
         for r in range(4):
             nc.sync.dma_start(plane_late[r:P:32, :], got_late[P - ROWS + r : P : 4, :])
         nc.sync.dma_start(dw_raw[1][:], dw_rows[:, :, HALF:])
-        w4_plane = w4_rows[:].bitcast(U8)
+        w4_plane = plane_early[:].bitcast(U8)[:, EARLY:]
 
         def tab_plane(g, j):
             m = g * S + j * P

@@ -71,7 +71,7 @@ def tile_list_tabbag_tm_sum_silu_kernel(tc, tab, w4_words, w4_scales, dw, b, off
         nc.vector.tensor_copy(staged[96:P, 0 : EARLY // 4], got_early[96:P, :])
         for r in range(4):
             nc.sync.dma_start(plane_early[r:P:32, :], staged[P - ROWS + r : P : 4, :])
-        got_late = reuse.tile([P, LATE // 4], I32, name="got_late", offset=0)
+        got_late = reuse.tile([P, LATE // 4], I32, name="got_late", offset=32)
         nc.vector.tensor_copy(got_late[:].bitcast(U8), scale_window.indirect(list_slice(EARLY, LATE)))
         dw_raw = [reuse.tile([P, PACK, HALF], F32, name="dw_raw%d" % h, offset=(h + 1) * RAW) for h in range(2)]
         dw_rows = dw.rearrange("(p i) n -> p i n", i=PACK)
@@ -91,13 +91,16 @@ def tile_list_tabbag_tm_sum_silu_kernel(tc, tab, w4_words, w4_scales, dw, b, off
         nc.scalar.activation(table_warm[:], ident[:, 0:1], SILU)
         b_turned = ps.tile([P, P], F32, name="b_turned", offset=6 * BANK)
         nc.tensor.transpose(b_turned[:], b_rows[:], ident[:])
-        b_col = reuse.tile([P, 2], F32, name="b_col", offset=SCALES_AT)
+        b_col = reuse.tile([P, 2], F32, name="b_col", offset=0)
         nc.scalar.copy(b_col[:], b_turned[:, P - 2 : P])
         b_ps = ps.tile([P, M], F32, name="b_ps", offset=7 * BANK)
         for h in range(2):
             nc.tensor.transpose(b_ps[:, h * P : (h + 1) * P], b_col[:, h : h + 1].to_broadcast([P, P]), ident[:])
         bias = sb.tile([P, M], F32, name="bias")
         nc.scalar.copy(bias[:], b_ps[:])
+        clock_warm = ps.tile([P, P], F32, name="clock_warm", offset=6 * BANK)
+        for turn in range(5):
+            nc.tensor.transpose(clock_warm[:], bias[:, 0:P], ident[:])
 
         acc = [
             [ps.tile([P, HALF], F32, name="acc%d_%d" % (h, j), offset=(h * TILES + j) * BANK) for j in range(TILES)]

@@ -21,7 +21,7 @@ PACK = 4
 HALF = 128
 ROWS = 16
 PIECE = 256
-EARLY = S + PIECE
+EARLY = 2 * S
 LATE = G * S - EARLY
 BANK = 2048
 RAW = PACK * HALF * 4
@@ -46,6 +46,7 @@ def tile_list_tabbag_tm_sum_silu_kernel(tc, tab, w4_words, w4_scales, dw, b, off
         nc.scalar.dma_start(staged[P - ROWS : P, EARLY // 4 :], w4_scales[0].bitcast(I32))
         b_rows = sb.tile([P, P], F32, name="b_rows")
         nc.scalar.dma_start(b_rows[P - 2 : P, :], b.rearrange("(h n) -> h n", h=2))
+        nc.vector.memset(b_rows[0 : P - 2, :], 0.0)
         nc.vector.memset(tab_scales[0 : P - ROWS, :], 0)
 
         tab_words = sb.tile([P, T], I32, name="tab_words", align_bytes=64)
@@ -53,7 +54,6 @@ def tile_list_tabbag_tm_sum_silu_kernel(tc, tab, w4_words, w4_scales, dw, b, off
         w4_codes = sb.tile([P, 2 * M // 4], I32, name="w4_codes", align_bytes=64)
         nc.sync.dma_start(w4_codes[:], w4_words[0].bitcast(I32))
 
-        nc.gpsimd.memset(b_rows[0 : P - 2, :], 0.0)
         ident = sb.tile([P, P], F32, name="ident")
         make_identity(nc, ident[:])
 
@@ -70,15 +70,15 @@ def tile_list_tabbag_tm_sum_silu_kernel(tc, tab, w4_words, w4_scales, dw, b, off
         nc.vector.tensor_copy(got_early[:].bitcast(U8), scale_window.indirect(list_slice(0, EARLY)))
         nc.vector.tensor_copy(staged[96:P, 0 : EARLY // 4], got_early[96:P, :])
         for r in range(4):
-            nc.sync.dma_start(plane_early[r:P:32, :], staged[P - ROWS + r : P : 4, :])
+            (nc.sync, nc.scalar)[r % 2].dma_start(plane_early[r:P:32, :], staged[P - ROWS + r : P : 4, :])
         got_late = reuse.tile([P, LATE // 4], I32, name="got_late", offset=32)
         nc.vector.tensor_copy(got_late[:].bitcast(U8), scale_window.indirect(list_slice(EARLY, LATE)))
         dw_raw = [reuse.tile([P, PACK, HALF], F32, name="dw_raw%d" % h, offset=(h + 1) * RAW) for h in range(2)]
         dw_rows = dw.rearrange("(p i) n -> p i n", i=PACK)
-        nc.sync.dma_start(dw_raw[0][:], dw_rows[:, :, 0:HALF])
+        for h in range(2):
+            nc.sync.dma_start(dw_raw[h][:], dw_rows[:, :, h * HALF : (h + 1) * HALF])
         for r in range(4):
             nc.sync.dma_start(plane_late[r:P:32, :], got_late[P - ROWS + r : P : 4, :])
-        nc.sync.dma_start(dw_raw[1][:], dw_rows[:, :, HALF:])
         w4_plane = plane_early[:].bitcast(U8)[:, EARLY:]
 
         def tab_plane(g, j):
@@ -87,8 +87,8 @@ def tile_list_tabbag_tm_sum_silu_kernel(tc, tab, w4_words, w4_scales, dw, b, off
                 return plane_early[:].bitcast(U8)[:, m : m + P]
             return plane_late[:].bitcast(U8)[:, m - EARLY : m - EARLY + P]
 
-        table_warm = sb.tile([P, 1], F32, name="table_warm")
-        nc.scalar.activation(table_warm[:], ident[:, 0:1], SILU)
+        table_warm = sb.tile([P // 2, 1], F32, name="table_warm")
+        nc.scalar.activation(table_warm[:], b_rows[0 : P // 2, 0:1], SILU)
         b_turned = ps.tile([P, P], F32, name="b_turned", offset=6 * BANK)
         nc.tensor.transpose(b_turned[:], b_rows[:], ident[:])
         b_col = reuse.tile([P, 2], F32, name="b_col", offset=0)
@@ -100,7 +100,7 @@ def tile_list_tabbag_tm_sum_silu_kernel(tc, tab, w4_words, w4_scales, dw, b, off
         nc.scalar.copy(bias[:], b_ps[:])
         clock_warm = ps.tile([P, P], F32, name="clock_warm", offset=6 * BANK)
         for turn in range(5):
-            nc.tensor.transpose(clock_warm[:], bias[:, 0:P], ident[:])
+            nc.tensor.transpose(clock_warm[:], b_rows[:], ident[:])
 
         acc = [
             [ps.tile([P, HALF], F32, name="acc%d_%d" % (h, j), offset=(h * TILES + j) * BANK) for j in range(TILES)]

@@ -27,6 +27,7 @@ BANK = 2048
 RAW = PACK * HALF * 4
 SCALES_AT = 3 * RAW
 TILES = S // P
+WARM = 512
 
 
 def tile_list_tabbag_tm_sum_silu_kernel(tc, tab, w4_words, w4_scales, dw, b, offs, out):
@@ -71,7 +72,7 @@ def tile_list_tabbag_tm_sum_silu_kernel(tc, tab, w4_words, w4_scales, dw, b, off
         nc.vector.tensor_copy(staged[96:P, 0 : EARLY // 4], got_early[96:P, :])
         for r in range(4):
             (nc.sync, nc.scalar)[r % 2].dma_start(plane_early[r:P:32, :], staged[P - ROWS + r : P : 4, :])
-        got_late = reuse.tile([P, LATE // 4], I32, name="got_late", offset=32)
+        got_late = reuse.tile([P, LATE // 4], I32, name="got_late", align_bytes=64, offset=64)
         nc.vector.tensor_copy(got_late[:].bitcast(U8), scale_window.indirect(list_slice(EARLY, LATE)))
         dw_raw = [reuse.tile([P, PACK, HALF], F32, name="dw_raw%d" % h, offset=(h + 1) * RAW) for h in range(2)]
         dw_rows = dw.rearrange("(p i) n -> p i n", i=PACK)
@@ -99,8 +100,19 @@ def tile_list_tabbag_tm_sum_silu_kernel(tc, tab, w4_words, w4_scales, dw, b, off
         bias = sb.tile([P, M], F32, name="bias")
         nc.scalar.copy(bias[:], b_ps[:])
         clock_warm = ps.tile([P, P], F32, name="clock_warm", offset=6 * BANK)
-        for turn in range(5):
+        for turn in range(3):
             nc.tensor.transpose(clock_warm[:], b_rows[:], ident[:])
+        mx_warm = ps.tile([P, WARM], F32, name="mx_warm", offset=6 * BANK)
+        nc.tensor.matmul_mx(
+            out=mx_warm[:],
+            lhsT=tab_words[:, 0:P].bitcast(FP8X4),
+            lhsT_scale=got_late[:].bitcast(U8)[:, 0:P],
+            rhs=tab_words[:, 0:WARM].bitcast(FP8X4),
+            rhs_scale=got_late[:].bitcast(U8)[:, 0:WARM],
+            start=True,
+            stop=True,
+        )
+
 
         acc = [
             [ps.tile([P, HALF], F32, name="acc%d_%d" % (h, j), offset=(h * TILES + j) * BANK) for j in range(TILES)]

from contextlib import ExitStack

import concourse.mybir as mybir
from concourse.masks import make_identity

G, K, M, T, S = 3, 512, 256, 4096, 512
FLOPS = 2 * 2 * G * K * M * S

F32 = mybir.dt.float32
BF16 = mybir.dt.bfloat16
I32 = mybir.dt.int32
U32 = mybir.dt.uint32
U16 = mybir.dt.uint16
U8 = mybir.dt.uint8
FP8X4 = mybir.dt.float8_e4m3fn_x4
FP4X4 = mybir.dt.float4_e2m1fn_x4
SILU = mybir.ActivationFunctionType.Silu

P = 128
PACK = 4
HALF = 128
ROWS = 16
PIECE = 256
EARLY = 2 * S
LATE = G * S - EARLY
BANK = 2048
RAW = PACK * HALF * 4
SCALES_AT = 3 * RAW
TILES = S // P
WARM = 512


def tile_list_tabbag_tm_sum_silu_kernel(tc, tab, w4_words, w4_scales, dw, b, offs, out):
    nc = tc.nc
    with ExitStack() as ctx:
        sb = ctx.enter_context(tc.tile_pool(name="sb", bufs=1))
        reuse = ctx.enter_context(tc.tile_pool(name="reuse", bufs=1))
        ps = ctx.enter_context(tc.psum_pool(name="ps", bufs=1))

        tab_scales = reuse.tile([P, T // 4], I32, name="tab_scales", align_bytes=64, offset=SCALES_AT)
        nc.sync.dma_start(
            tab_scales[P - ROWS : P, :], tab[0, K * T :].rearrange("(q t) -> q t", q=ROWS).bitcast(I32)
        )
        offsets = sb.tile([P, G * S // 16], U16, name="offsets")
        nc.sync.dma_start(offsets[:], offs)
        staged = sb.tile([P, (EARLY + M) // 4], I32, name="staged")
        nc.scalar.dma_start(staged[P - ROWS : P, EARLY // 4 :], w4_scales[0].bitcast(I32))
        b_rows = sb.tile([P, P], F32, name="b_rows")
        nc.scalar.dma_start(b_rows[P - 2 : P, :], b.rearrange("(h n) -> h n", h=2))
        nc.vector.memset(b_rows[0 : P - 2, :], 0.0)
        nc.vector.memset(tab_scales[0 : P - ROWS, :], 0)

        tab_words = sb.tile([P, T], I32, name="tab_words", align_bytes=64)
        nc.sync.dma_start(tab_words[:], tab[0, 0 : K * T].rearrange("(p x) -> p x", p=P).bitcast(I32))
        w4_codes = sb.tile([P, 2 * M // 4], I32, name="w4_codes", align_bytes=64)
        nc.sync.dma_start(w4_codes[:], w4_words[0].bitcast(I32))

        ident = sb.tile([P, P], F32, name="ident")
        make_identity(nc, ident[:])

        plane_early = sb.tile([P, (EARLY + M) // 4], I32, name="plane_early", align_bytes=64)
        nc.vector.memset(plane_early[:], 0)
        plane_late = sb.tile([P, LATE // 4], I32, name="plane_late", align_bytes=64)
        nc.vector.memset(plane_late[:], 0)
        scale_window = tab_scales[:].bitcast(U8)

        def list_slice(first, count):
            return offsets[:, first // 16 : (first + count) // 16]

        got_early = reuse.tile([P, EARLY // 4], I32, name="got_early", offset=0)
        nc.vector.tensor_copy(got_early[:].bitcast(U8), scale_window.indirect(list_slice(0, EARLY)))
        nc.vector.tensor_copy(staged[96:P, 0 : EARLY // 4], got_early[96:P, :])
        for r in range(4):
            (nc.sync, nc.scalar)[r % 2].dma_start(plane_early[r:P:32, :], staged[P - ROWS + r : P : 4, :])
        got_late = reuse.tile([P, LATE // 4], I32, name="got_late", align_bytes=64, offset=64)
        nc.vector.tensor_copy(got_late[:].bitcast(U8), scale_window.indirect(list_slice(EARLY, LATE)))
        dw_raw = [reuse.tile([P, PACK, HALF], F32, name="dw_raw%d" % h, offset=(h + 1) * RAW) for h in range(2)]
        dw_rows = dw.rearrange("(p i) n -> p i n", i=PACK)
        for h in range(2):
            nc.sync.dma_start(dw_raw[h][:], dw_rows[:, :, h * HALF : (h + 1) * HALF])
        for r in range(4):
            nc.sync.dma_start(plane_late[r:P:32, :], got_late[P - ROWS + r : P : 4, :])
        w4_plane = plane_early[:].bitcast(U8)[:, EARLY:]

        def tab_plane(g, j):
            m = g * S + j * P
            if m < EARLY:
                return plane_early[:].bitcast(U8)[:, m : m + P]
            return plane_late[:].bitcast(U8)[:, m - EARLY : m - EARLY + P]

        table_warm = sb.tile([P // 2, 1], F32, name="table_warm")
        nc.scalar.activation(table_warm[:], b_rows[0 : P // 2, 0:1], SILU)
        b_turned = ps.tile([P, P], F32, name="b_turned", offset=6 * BANK)
        nc.tensor.transpose(b_turned[:], b_rows[:], ident[:])
        b_col = reuse.tile([P, 2], F32, name="b_col", offset=0)
        nc.scalar.copy(b_col[:], b_turned[:, P - 2 : P])
        b_ps = ps.tile([P, M], F32, name="b_ps", offset=7 * BANK)
        for h in range(2):
            nc.tensor.transpose(b_ps[:, h * P : (h + 1) * P], b_col[:, h : h + 1].to_broadcast([P, P]), ident[:])
        bias = sb.tile([P, M], F32, name="bias")
        nc.scalar.copy(bias[:], b_ps[:])
        clock_warm = ps.tile([P, P], F32, name="clock_warm", offset=6 * BANK)
        for turn in range(3):
            nc.tensor.transpose(clock_warm[:], b_rows[:], ident[:])
        mx_warm = ps.tile([P, WARM], F32, name="mx_warm", offset=6 * BANK)
        nc.tensor.matmul_mx(
            out=mx_warm[:],
            lhsT=tab_words[:, 0:P].bitcast(FP8X4),
            lhsT_scale=got_late[:].bitcast(U8)[:, 0:P],
            rhs=tab_words[:, 0:WARM].bitcast(FP8X4),
            rhs_scale=got_late[:].bitcast(U8)[:, 0:WARM],
            start=True,
            stop=True,
        )


        acc = [
            [ps.tile([P, HALF], F32, name="acc%d_%d" % (h, j), offset=(h * TILES + j) * BANK) for j in range(TILES)]
            for h in range(2)
        ]
        words = {}
        dw_codes = [sb.tile([P, HALF], U32, name="dw_codes%d" % h, align_bytes=64) for h in range(2)]
        dw_plane = [sb.tile([P, HALF], U8, name="dw_plane%d" % h, align_bytes=64) for h in range(2)]

        def gather_words(g, u):
            if g < G - 1:
                piece = sb.tile([P, PIECE], U32, name="words%d_%d" % (g, u), align_bytes=64)
            else:
                piece = reuse.tile([P, PIECE], U32, name="words_last%d" % u, align_bytes=64, offset=RAW + u * PIECE * 4)
            nc.vector.tensor_copy(piece[:], tab_words[:].bitcast(U32).indirect(list_slice(g * S + u * PIECE, PIECE)))
            for e in range(PIECE // P):
                words[g, u * (PIECE // P) + e] = piece[:, e * P : (e + 1) * P].bitcast(FP8X4)

        def quantise_dw(h):
            dw_bf = sb.tile([P, HALF, PACK], BF16, name="dw_bf%d" % h, align_bytes=64)
            nc.scalar.copy(
                dw_bf[:].rearrange("p (c e) i -> p c i e", e=4), dw_raw[h][:].rearrange("p i (c e) -> p c i e", e=4)
            )
            nc.vector.quantize_mx(
                out=dw_codes[h][:].bitcast(FP8X4), scales=dw_plane[h][:], in_=dw_bf[:].rearrange("p n i -> p (n i)")
            )

        def mx_pass(g, j, h, codes, plane, start, stop):
            nc.tensor.matmul_mx(
                out=acc[h][j][:],
                lhsT=words[g, j],
                lhsT_scale=tab_plane(g, j),
                rhs=codes,
                rhs_scale=plane,
                start=start,
                stop=stop,
            )

        def w4_pass(g, j, h):
            codes = w4_codes[:].bitcast(U8)[:, 2 * h * HALF : 2 * (h + 1) * HALF].bitcast(FP4X4)
            mx_pass(g, j, h, codes, w4_plane[:, h * HALF : (h + 1) * HALF], g == 0, False)

        def dw_pass(g, j, h):
            mx_pass(g, j, h, dw_codes[h][:].bitcast(FP8X4), dw_plane[h][:], False, g == G - 1)

        def finish(j, h, step):
            res = sb.tile([P, HALF], F32, name="res%d_%d" % (h, j))
            for c in range(0, HALF, step):
                if h == 0:
                    y = reuse.tile([P, step], F32, name="y_first%d" % j, offset=2 * RAW + j * HALF * 4)
                else:
                    y = sb.tile([P, step], F32, name="y%d_%d" % (j, c))
                nc.vector.tensor_tensor(
                    y[:], acc[h][j][:, c : c + step], bias[:, h * HALF + c : h * HALF + c + step], mybir.AluOpType.add
                )
                nc.scalar.activation(res[:, c : c + step], y[:], SILU)
            nc.sync.dma_start(out[j * P : (j + 1) * P, h * HALF : (h + 1) * HALF], res[:])

        for u in range(S // PIECE):
            for g in range(G - 1):
                gather_words(g, u)
                for j in range(2 * u, 2 * u + 2):
                    for h in range(2):
                        w4_pass(g, j, h)
        quantise_dw(0)
        for j in range(TILES):
            for g in range(G - 1):
                dw_pass(g, j, 0)
        for u in range(S // PIECE):
            gather_words(G - 1, u)
        quantise_dw(1)
        for u in range(S // PIECE):
            for j in range(2 * u, 2 * u + 2):
                w4_pass(G - 1, j, 0)
                dw_pass(G - 1, j, 0)
                finish(j, 0, HALF)
            for j in range(2 * u, 2 * u + 2):
                w4_pass(G - 1, j, 1)
        for j in range(TILES):
            for g in range(G):
                dw_pass(g, j, 1)
            finish(j, 1, HALF // 2 if j == TILES - 1 else HALF)
